import numpy as np, ml_dtypes
CORES = [6,15,38,47]
N = 4
BF = ml_dtypes.bfloat16
def gentries(a):
    return np.ascontiguousarray(a.reshape(8, 16, -1).transpose(0, 2, 1)).reshape(8, -1)
def gtable(e):
    e = np.asarray(e); return np.ascontiguousarray(e.reshape(8, -1, 16).transpose(0, 2, 1)).reshape(128, -1).astype(np.int32)
V, GH, RO, DF, TR, FQ = 4096, 256, 6, 16, 9, 4
NS, NU = V // 16, V // 256; S = NS + NU + 1; W = V + (N - 1) * GH
LO, HI = DF + 2, 2 * DF + 1
SMALL = (0, 0, 1, 2, 3, 7, 14, 15, 16)
def parts(rng, share):
    x = rng.integers(LO, HI + 1, (N, 8, 16, V)); xb = rng.integers(LO, HI + 1, (N, 8, 16, V))
    a = np.where(rng.random((N, 8, V)) < share, rng.integers(V, W, (N, 8, V)), rng.integers(0, V, (N, 8, V)))
    return x, xb, a, np.zeros((N, 8, S), np.int64), np.full((N, 8, S), 16, np.int64)
def tame(a):
    k = np.where(a >= V, (a - V) % GH, 0)
    return np.where(a >= V, a - k + k % 14, np.where((a == 14) | (a == 15), 0, a))
def pack(x, xb, a, sg, lm):
    return {"x0": np.ascontiguousarray(x.reshape(N, 128, V)).astype(np.float32).astype(BF), "xi": np.ascontiguousarray(xb.reshape(N, 128, V)).astype(np.float32).astype(BF),
            "ad": np.stack([gtable(e) for e in a]), "sg": np.asarray(sg).astype(np.int32), "lm": np.asarray(lm).astype(np.int32)}
def lows(rng, x, xb, a, n):
    o = rng.permutation(V)[:n]; t = rng.choice(np.array([TR - 1, TR, TR + 1, 16, 16]), n)
    m = np.argsort(rng.random((16, n)), axis=0) < t
    x[:, o] = np.where(m, rng.integers(0, 4, (16, n)), x[:, o]); xb[:, o] = np.where(m, rng.integers(0, 4, (16, n)), xb[:, o])
    h = n // 2; a[o[:h]] = np.where(rng.random(h) < 0.5, o[:h], rng.permutation(o[:h]))
def trigger(rng, x, a, sg, lm):
    s = NS - 1 if rng.random() < 0.5 else int(rng.integers(1, NS))
    lm[:NS] = rng.choice(np.array([13, 14, 16]), NS); lm[s] = rng.integers(0, 5); lm[NS + s // 16] = 0; lm[S - 1] = 0
    for i in range(5):
        v = 16 * s + 3 * i; e = rng.integers(0, 4, 16)
        x[:, v + 2] = e; x[:, v + 1] = e + DF; x[:, v] = e + 2 * DF; a[v] = v + 1; a[v + 1] = v + 2; a[v + 2] = v + 2
    a[16 * s + 15] = 16 * s + 15
def plant(rng, x, xb, a, cr, mode, keep, near):
    x[:, 15] = 2; xb[:, 15] = 2; x[:, 14] = LO; xb[:, 14] = LO; a[14:16] = 15
    if mode == 2: x[:, 15] = LO; x[:, 14] = 1; xb[:, 14] = 1; a[14:16] = 14
    to = 14 if mode == 3 else 15
    o = np.flatnonzero(cr); n = len(o); t = rng.choice(np.array([TR, TR, TR + 1, 16]), n)
    st = np.where(np.argsort(rng.random((16, n)), axis=0) < t, rng.integers(LO + 1, HI + 1, (16, n)), LO)
    x[:, o] = st; xb[:, o] = st if keep else LO; a[o] = to
    o = rng.permutation(np.flatnonzero(~cr[16:]) + 16)[:near]; n = len(o)
    x[:, o] = np.where(np.argsort(rng.random((16, n)), axis=0) < TR - 1, rng.integers(LO + 1, HI + 1, (16, n)), LO); a[o] = to
    if mode == 2: xb[:, o] = x[:, o]
def strike(rng, x, a, lm, s, t):
    n = (1, 1, 2, 3, 5, 8, 13)[t - 1]
    a[(a >> 4) == s] = 0; v = 16 * s + np.arange(16); a[v] = v
    p = 16 * s + rng.permutation(16)[:n + 1]; e = rng.integers(0, 4, 16)
    x[:, p] = (e + DF)[:, None]; x[:, p[0]] = e + 2 * DF; x[:, p[n]] = e; a[p[:n]] = p[1:]
    lm[s] = 0; lm[NS + s // 16] = 0; lm[S - 1] = 0
def setup_inputs(rng):
    x, xb, a, sg, lm = parts(rng, 0.06); order = rng.permutation(N)
    mix = ((0.9, 0.07, 0.03), (0.75, 0.15, 0.1), (0.95, 0.03, 0.02), (0.6, 0.25, 0.15))
    for q in range(N):
        n = FQ if q == order[0] else FQ - 1 if q == order[1] else int(rng.integers(0, FQ - 1))
        weak = rng.permutation(8)[:n]
        for g in range(8):
            sg[q, g] = rng.choice(3, S, p=mix[int(rng.integers(0, 4))])
            lm[q, g, :NS] = rng.choice(np.array([3, 4, 6, 8, 10, 13, 16]), NS); lm[q, g, NS:NS + NU] = rng.choice(np.array([1, 2, 4, 8, 16]), NU)
            lows(rng, x[q, g], xb[q, g], a[q, g], (V // 512, V // 128, V // 64)[int(rng.integers(0, 3))])
            if np.any(weak == g): trigger(rng, x[q, g], a[q, g], sg[q, g], lm[q, g])
    return pack(x, xb, a, sg, lm)
def setup_inputs_spread(rng):
    x, xb, a, sg, lm = parts(rng, 0.12)
    x = np.minimum((np.exp2(6 * rng.random((N, 8, 1, V))) * rng.random((N, 8, 16, V))).astype(np.int64), 63)
    xb = np.minimum((np.exp2(6 * rng.random((N, 8, 1, V))) * rng.random((N, 8, 16, V))).astype(np.int64), 63)
    for q in range(N):
        o = rng.permutation(8); k = rng.permutation(8)[:FQ - 1]
        for i in range(8):
            g = int(o[i])
            if i % 2: a[q, g] = np.where(a[q, g] < V, (V * rng.random(V) ** 3).astype(np.int64), a[q, g])
            if i < 4: sg[q, g] = rng.choice(3, S, p=(0.97, 0.02, 0.01))
            else: sg[q, g] = rng.choice(3, S, p=(0.6, 0.25, 0.15)); lm[q, g, :S - 1] = rng.integers(0, 17, S - 1)
            if np.any(k == g): lm[q, g, S - 1] = rng.integers(0, 4)
    return pack(x, xb, a, sg, lm)
def setup_inputs_ends(rng):
    x, xb, a, sg, lm = parts(rng, 0.15)
    def both():
        t = rng.choice(np.array([0, 0, TR - 1, TR, TR + 1, 16, 16]), (N, 8, V, 1))
        return np.ascontiguousarray((63 * (np.argsort(rng.random((N, 8, V, 16)), axis=3) < t)).transpose(0, 1, 3, 2))
    x = both(); xb = both()
    u = rng.random((N, 8, V)); a = np.where(u < 0.36, 0, np.where(u < 0.72, W - 1, a))
    z = 63 * rng.integers(0, 2, (N, 8, 1)); z[:, 7] = 0; x[..., 0] = z; xb[..., 0] = z
    sg = 2 * (rng.random((N, 8, S)) < rng.choice(np.array([0.1, 0.5]), (N, 8, 1))).astype(np.int64)
    lm = 16 * (rng.random((N, 8, S)) < rng.choice(np.array([0.5, 0.9]), (N, 8, 1))).astype(np.int64)
    lm[..., S - 1] = 16; sg[..., S - 1] = 2 * (rng.random((N, 8)) < 0.25)
    x[:, 7, :, V - 16:] = 63; xb[:, 7, :, V - 16:] = 63; a[:, 7, V - 16:] = 0; a[:, 7, 0] = 0; lm[:, 7, NS - 1] = 16
    for q in range(N):
        k = rng.permutation(7)[:FQ if q == N - 1 else FQ - 1]
        for g in k:
            lm[q, g, S - 1] = 0
            if q == N - 1:
                lm[q, g, NS:NS + NU] = 0; x[q, g, :, 0] = 0; xb[q, g] = 0; xb[q, g, :, V - 16:] = 63
                u = rng.random(V); a[q, g] = np.where(u < 0.86, 0, np.where(u < 0.93, V - 1, rng.integers(0, V, V)))
                a[q, g, 0] = 0; a[q, g, V - 16:] = V - 1
    return pack(x, xb, a, sg, lm)
def pair(rng, die, top):
    if die:
        c = int(rng.integers(0, top)); return c, (top if rng.random() < 0.3 else c + 1)
    c = SMALL[int(rng.integers(0, 9))]; return c, min(c if rng.random() < 0.5 else 0, top)
def setup_inputs_corners(rng):
    x, xb, a, sg, lm = parts(rng, 0.05); a = tame(a); sg = rng.integers(0, 3, (N, 8, S)); order = rng.permutation(N); more = int(rng.integers(FQ + 1, 8))
    for i in range(N):
        q = int(order[i]); mode = (3, 1, 2, 3, 3, 1, 1, 2)[i]; o = rng.permutation(8); dg = o[:(FQ, FQ - 1, more, 0, 7, 8, FQ, FQ - 1)[i]]
        full = int(o[0]) if i in (0, 6) else -1; stay = int(o[FQ - 1]) if i in (1, 7) else -1; late = int(o[FQ]) if i == 1 else -1
        hit = i in (0, 2, 4, 5, 6)
        for k in range(8):
            g = int(o[k]); early = bool(np.any(dg == g)); die = early or g == late; cr = np.zeros(V, bool)
            wild = k in (5, 6); part = not (hit or die or wild or g == stay)
            when = 3 if i in (1, 7) and not early and g != stay else mode
            lm[q, g, S - 1], n = pair(rng, die, NU)
            if g == full: lm[q, g, S - 1] = NU - 1; n = NU
            elif g == stay: lm[q, g, S - 1] = 16 if rng.random() < 0.5 else NU; n = NU
            elif k == 7 and not die: n = 0
            du = rng.permutation(NU)[:n]
            for j in range(NU):
                top = 15 if j == 0 else 16
                lm[q, g, NS + j], n = pair(rng, bool(np.any(du == j)), top); ds = 16 - top + rng.permutation(top)[:n]
                for s in range(16 - top, 16):
                    lm[q, g, 16 * j + s], n = pair(rng, bool(np.any(ds == s)), 16)
                    cr[256 * j + 16 * s + rng.permutation(16)[:n]] = True
            if part and k == 7: cr[:] = False
            if wild: a[q, g] = np.where(a[q, g] == 13, 0, a[q, g])
            plant(rng, x[q, g], xb[q, g], a[q, g], cr, when, k == 5, 0 if part or (i == 1 and when == 1) else V // 32)
            if wild:
                x[q, g, :, 13] = LO if hit else HI; xb[q, g, :, 13] = HI; a[q, g, 13] = 15 if hit else 14
            elif g != stay:
                xb[q, g, :, 14 if when == 2 else 15] = LO
            if part and k < 7:
                m = ~cr & (a[q, g] < V); m[14:16] = False
                e = V + GH * rng.integers(0, N - 1, V) + rng.integers(0, 14, V)
                a[q, g] = np.where(m, np.where(rng.random(V) < 0.5, np.arange(V), e), a[q, g])
    return pack(x, xb, a, sg, lm)
def setup_inputs_crowd(rng):
    x, xb, a, sg, lm = parts(rng, 0.06); a = tame(a)
    for q in range(N):
        o = rng.permutation(8)
        for g in range(8):
            k = int(o[g]); cr = np.zeros(V, bool)
            if k in (0, 1): a[q, g] = V - 1
            if k == 4: a[q, g] = W - 1
            if k == 5: a[q, g] = rng.choice(np.array([0, V - 1, V, W - 1, 7]), V)
            if k in (1, 2, 3, 6):
                for j in range(NU):
                    c = int(rng.integers(0, 4)); lm[q, g, 16 * j:16 * j + 16] = (15, 14, 15, 16)[c]
                    if c == 2: lm[q, g, 16 * j + int(rng.integers(0, 16))] = 16
                lm[q, g, NS:NS + NU] = rng.choice(np.array([14, 15, 16]), NU); lm[q, g, S - 1] = (0, NU // 2, NU - 1)[int(rng.integers(0, 3))]
                sg[q, g] = rng.integers(0, 3, S)
            if k == 1:
                cr[V - 2] = True; sg[q, g, NS - 1] = 2; lm[q, g, NS - 1] = 16
            if k in (2, 3, 6): cr[:] = True; cr[14:16] = False
            if k == 3: s = np.arange(1, NS, 2); cr[16 * s + rng.integers(0, 16, len(s))] = False
            if k == 6: cr[int(rng.integers(16, V))] = False
            if k in (1, 2, 3, 6): plant(rng, x[q, g], xb[q, g], a[q, g], cr, 1 if k in (2, 3) else 3, k == 3, 0)
    return pack(x, xb, a, sg, lm)
def setup_inputs_calm(rng):
    x, xb, a, sg, lm = parts(rng, 0.04); a = tame(a)
    late = (5, min(RO - 1, 7))[:RO - 5]; hit = rng.permutation(N)[:len(late)]
    for q in range(N):
        o = rng.permutation(8); used = np.zeros((8, NS), bool)
        for g in range(8):
            k = int(o[g])
            if k == 0: continue
            sup = 1 + rng.permutation(NS - 2)[:NS // 10]; sup[0] = NS - 1; c1 = np.zeros(V, bool); c3 = np.zeros(V, bool)
            used[g, sup] = True
            for j in range(len(sup)):
                s = int(sup[j]); n = 1 + j % 3; w = 16 * s + rng.permutation(16)[:n]
                if k in (1, 4, 6) or (k == 3 and (j >> 1) & 1): c1[w] = True
                else: c3[w] = True
                sg[q, g, s] = 2 if k == 4 else (2, 1, 0, 2, 1)[j % 5]
                if k in (6, 7): lm[q, g, s] = n - 1 + ((j // 3) & 1)
            if k == 6: lm[q, g, NS:NS + NU] = rng.integers(0, 4, NU); sg[q, g, NS:NS + NU] = rng.integers(0, 3, NU)
            if np.any(c1): plant(rng, x[q, g], xb[q, g], a[q, g], c1, 1, k in (4, 6), 0)
            if np.any(c3): plant(rng, x[q, g], xb[q, g], a[q, g], c3, 3, k == 5, 0)
        for i in range(len(late)):
            if int(hit[i]) != q: continue
            for g in range(8):
                if int(o[g]) >= FQ: continue
                s = int(rng.choice(np.flatnonzero(~used[g, GH // 16:]) + GH // 16))
                strike(rng, x[q, g], a[q, g], lm[q, g], s, late[i])
    return pack(x, xb, a, sg, lm)
def check_inputs(d):
    bad = []
    for k, lo, hi in (("x0", 0, 63), ("xi", 0, 63), ("ad", 0, W - 1), ("sg", 0, 2), ("lm", 0, 16)):
        v = np.asarray(d[k]).astype(np.float64)
        if not np.all((v >= lo) & (v <= hi) & (v == np.rint(v))): bad.append("range of " + k)
    return bad
def judge(c, s, m):
    n = np.add.reduce(c.astype(np.int64), axis=-1); die = n > m
    rest = np.add.accumulate(c.astype(np.int64), axis=-1) > 0
    b = np.where((s == 0)[..., None], c, np.where((s == 1)[..., None], rest, (n > 0)[..., None]))
    return b | die[..., None], die
def reference(x0, xi, ad, sg, lm):
    x = x0.astype(np.float32).astype(np.int16).reshape(N, 8, 16, V); xb = xi.astype(np.float32).astype(np.int16).reshape(N, 8, 16, V)
    a0 = np.stack([gentries(e) for e in ad]).astype(np.int64)
    s = sg.astype(np.int64); m = lm.astype(np.int64)
    a = a0; c = np.zeros_like(a0)
    u = np.full_like(a0, -1); w = np.zeros_like(a0)
    inc = np.ones_like(a0)
    for step in range(RO):
        seen = []
        for r in range(N):
            p = [x[r]]
            for d in range(1, N):
                q = (r - d) % N; p.append(x[q][(np.arange(8) + q - r) & 7][:, :, :GH])
            seen.append(np.concatenate(p, axis=2))
        y = np.take_along_axis(np.stack(seen), a[:, :, None, :], 3)
        own = a < V; ao = np.minimum(a, V - 1)
        ia = np.where(own, np.take_along_axis(inc, ao, 2), 0)
        crash = ((c > 0) & (c != ia)) | (np.add.reduce((y < x - DF).astype(np.int64), axis=2) >= TR)
        ua = np.take_along_axis(u, ao, 2); uc = np.take_along_axis(w, ao, 2); got = own & (ua >= 0)
        na = np.where(got, ua, a); nc = np.where(got, uc, c)
        b1, d1 = judge(crash.reshape(N, 8, NS, 16), s[:, :, :NS], m[:, :, :NS])
        b2, d2 = judge(d1.reshape(N, 8, NU, 16), s[:, :, NS:NS + NU], m[:, :, NS:NS + NU])
        b3, d3 = judge(d2.reshape(N, 8, 1, NU), s[:, :, S - 1:], m[:, :, S - 1:])
        rank = np.add.reduce(d3[:, :, 0].astype(np.int64), axis=1) >= FQ
        born = b1 | b2.reshape(N, 8, NS)[..., None] | np.repeat(b3[:, :, 0], 16, axis=2)[..., None] | rank[:, None, None, None]
        born = born.reshape(N, 8, V)
        x = np.where(born[:, :, None], xb, np.maximum(x, y))
        u = np.where(born, -1, a); w = np.where(born, 0, ia)
        a = np.where(born, a0, na); c = np.where(born, 0, nc)
        inc = inc + born
    return {"yx": np.ascontiguousarray(x.reshape(N, 128, V)).astype(np.float32).astype(BF), "ya": np.stack([gtable(e) for e in 16 * a + c]).astype(np.float32),
            "yu": np.stack([gtable(e) for e in np.where(u < 0, -1, 16 * u + w)]).astype(np.float32), "yi": np.stack([gtable(e) for e in inc]).astype(np.float32)}

@@ -1,0 +1,583 @@
+from concourse.bass import DstId, RemoteDMATransfer
+from concourse.mybir import AluOpType, AxisListType, ActivationFunctionType
+
+A = AluOpType
+F = ActivationFunctionType
+V, GH, W, STEPS, N = 4096, 256, 4864, 6, 4
+LW = W // 16
+BIG = 16384.0
+MAGIC = 201326592.0
+S0 = 2055.5
+
+SCRATCH = {
+    "xa": ("sbuf", [128, W], "bfloat16"), "xb": ("sbuf", [128, W], "bfloat16"),
+    "w2": ("sbuf", [128, GH + 2 * V], "bfloat16"), "mw": ("sbuf", [128, 2 * W], "bfloat16"),
+    "dd": ("sbuf", [128, V], "bfloat16"), "cm": ("sbuf", [128, V], "bfloat16"),
+    "rr": ("sbuf", [128, V], "bfloat16"), "xo": ("sbuf", [128, V], "bfloat16"), "go": ("sbuf", [128, V], "bfloat16"),
+    "adi": ("sbuf", [128, 256], "int32"), "sgi": ("sbuf", [128, 288], "int32"), "lmi": ("sbuf", [128, 288], "int32"),
+    "of1": ("sbuf", [128, 256], "uint16"), "of2": ("sbuf", [128, 256], "uint16"), "idx": ("sbuf", [128, 256], "uint16"),
+    "ofc": ("sbuf", [128, 16], "uint16"),
+    "s0": ("sbuf", [128, 256], "float32"),
+    "pt": ("sbuf", [128, 3 * LW], "bfloat16"), "pj": ("sbuf", [128, 3 * LW], "bfloat16"),
+    "bt": ("sbuf", [128, 8 * LW], "bfloat16"),
+    "cr": ("sbuf", [128, 256], "bfloat16"), "cr1": ("sbuf", [128, 256], "bfloat16"), "nbe": ("sbuf", [128, 256], "bfloat16"),
+    "t9": ("sbuf", [128, 256], "bfloat16"), "k16": ("sbuf", [128, 256], "bfloat16"), "dia": ("sbuf", [128, 256], "bfloat16"),
+    "rex": ("sbuf", [128, 256], "bfloat16"), "c16": ("sbuf", [128, 256], "bfloat16"),
+    "ic": ("sbuf", [128, 144], "bfloat16"), "icf": ("sbuf", [128, 16], "float32"), "pi": ("sbuf", [128, 4], "int32"),
+    "col": ("sbuf", [128, 32], "float32"), "oh": ("sbuf", [128, 16], "float32"),
+    "bs": ("sbuf", [128, 6 * 144], "bfloat16"), "ids": ("sbuf", [128, 9 * 128], "bfloat16"),
+    "ms": ("sbuf", [128, 8 * 128], "bfloat16"),
+    "jf": ("sbuf", [128, 7 * 288], "bfloat16"),
+    "th": ("sbuf", [128, 96], "float32"), "m13": ("sbuf", [128, 16], "bfloat16"),
+    "d1": ("sbuf", [128, 32], "bfloat16"), "bd": ("sbuf", [128, 32], "bfloat16"), "w3": ("sbuf", [128, 16], "bfloat16"),
+    "rs": ("sbuf", [128, 16], "bfloat16"), "n3": ("sbuf", [128, 4], "float32"), "ed": ("sbuf", [128, 8], "bfloat16"),
+    "sc": ("sbuf", [128, 4], "float32"), "v0": ("sbuf", [128, 48], "float32"), "ix0": ("sbuf", [128, 16], "uint16"),
+    "rw": ("sbuf", [128, 256], "bfloat16"),
+    "oa": ("sbuf", [128, 256], "float32"), "ou": ("sbuf", [128, 256], "float32"), "oi": ("sbuf", [128, 256], "float32"),
+}
+for _k in range(8):
+    SCRATCH["p%d" % _k] = ("psum", [128, 512], "float32")
+NDMA = 80
+SEMAPHORES = ["qv", "qs", "qt", "qg"] + ["dm%d" % k for k in range(NDMA)] + ["ar%d" % k for k in range(STEPS)] + ["lo%d" % k for k in range(STEPS)]
+
+SEL_V = 1920
+SEL_V_FIRST = 2304
+LAST_CUTS = (0, 512, 1280, 2176, 3072, 4096)
+BANKS = (5, 6, 7)
+OWN_DMA = ()
+ORDER = {
+    0: "H2 h3 h1 q0 H0 G1 x2 z2 z0 x3 G3 x0 x1 d3 d2 C3 F0 d6 y1 y0 C2 d7 a7 P0 y3 C6 n1 F2 up k1 p2 n0 a2 C7 y2 L4 k0 u5 L1 n3 m2 L0 k3 n2 L5 a3 k2 m3 a6 j1 m7 b0 q1 j2 m6 b5 M0 b4 M5 M4 j3 b1 M1 j4",
+    1: "z0 q0 F0 G2 z1 p0 G3 d4 d5 n0 C4 F1 C5 d6 p1 l1 k0 d7 C6 n1 n2 b1 C7 k1 n3 k2 l0 b0 l2 k3 M0 a4 j1 m4 a5 M1 b2 l3 m5 M2 a6 q1 j2 a7 m6 b3 j3 j4 m7 M3",
+}
+
+
+def rank_program(g, core, T, topo):
+    rank = T.rank_of(core)
+    if rank is None:
+        return
+    ops = []
+    Q = {"v": g.vector, "s": g.scalar, "t": g.tensor, "g": g, "y": g.sync}
+
+    def ap(name, c0=0, c1=None, step=1, p=128):
+        t = T[name]
+        c1 = t.shape[1] if c1 is None else c1
+        a = t[0:p, c0:c1:step] if step > 1 else t[0:p, c0:c1]
+        if name[0] == "p" and name[1].isdigit():
+            return a, [(name, 0, 512, None)]
+        return a, [(name, c0, c1, None)]
+
+    def ind(win, off):
+        return win[0].indirect(off[0]), win[1] + off[1]
+
+    def val(x):
+        return x[0] if isinstance(x, tuple) else x
+
+    def reg(*xs):
+        r = []
+        for x in xs:
+            if isinstance(x, tuple):
+                r += x[1]
+        return r
+
+    def emit(q, fn, rd, wr, kind="c", sem=None, n=0):
+        ops.append({"q": q, "fn": fn, "rd": rd, "wr": wr, "kind": kind, "sem": sem, "n": n, "need": False})
+
+    def ts(out, in0, s1, op0, s2=None, op1=None):
+        if op1 is None:
+            emit("v", lambda: g.vector.tensor_scalar(out[0], in0[0], val(s1), None, op0), reg(in0, s1), out[1])
+        else:
+            emit("v", lambda: g.vector.tensor_scalar(out[0], in0[0], val(s1), val(s2), op0, op1), reg(in0, s1, s2), out[1])
+
+    def tt(out, in0, in1, op):
+        emit("v", lambda: g.vector.tensor_tensor(out[0], in0[0], in1[0], op), reg(in0, in1), out[1])
+
+    def cp(out, in0):
+        emit("v", lambda: g.vector.tensor_copy(out[0], in0[0]), in0[1], out[1])
+
+    def fill(out, c):
+        emit("v", lambda: g.vector.memset(out[0], c), [], out[1])
+
+    def act(out, in0, func, bias=0.0, scale=1.0):
+        emit("s", lambda: g.scalar.activation(out[0], in0[0], func, bias=val(bias), scale=scale), reg(in0, bias), out[1])
+
+    def mm(out, l, r, start, stop):
+        emit("t", lambda: g.tensor.matmul(out[0], l[0], r[0], start, stop), reg(l, r), out[1])
+
+    def iota(out, pattern, base, cm):
+        if out[1][0][0] == "pi":
+            emit("g", lambda: g.iota(out[0], pattern, base, cm), [], out[1])
+        else:
+            emit("g", lambda: g.iota(out[0], pattern, base, cm, allow_small_or_imprecise_dtypes=True), [], out[1])
+
+    nd = [0]
+
+    def dmas(q, items):
+        sem = "dm%d" % nd[0]
+        nd[0] += 1
+        for o, i, rd, wr in items:
+            emit(q, (lambda o=o, i=i: Q[q].dma_start(o, i)), rd, wr, "d", sem, 16 * len(items))
+
+    def rot(rows):
+        k = rank * rows
+        return [(0, k, 8 * rows - k), (8 * rows - k, 0, k)] if k else [(0, 0, 8 * rows)]
+
+    def load(name, c0, src, s0, s1, rows=16):
+        return [(T[name][a:a + n, c0:c0 + s1 - s0], T[src][b:b + n, s0:s1], [], [(name, c0, c0 + s1 - s0, ("ld", a))]) for a, b, n in rot(rows)]
+
+    def store(dst, name, c0, c1):
+        return [(T[dst][b:b + n, c0:c1], T[name][a:a + n, c0:c1], [(name, c0, c1, None)], []) for a, b, n in rot(16)]
+
+    def torow(name, c0, row, regions):
+        return [(T.mw[row:128:16, r * W:(r + 1) * W], T[name][:, c0:c0 + LW], [(name, c0, c0 + LW, None)], [("mw", r * W, (r + 1) * W, row)]) for r in regions]
+
+    peers = [T.cores[(rank + d) % N] for d in range(1, N)]
+    mask = topo.mask(core, peers[0])
+    for c in peers[1:]:
+        mask &= topo.mask(core, c)
+    neng = bin(mask).count("1")
+
+    def exchange(k):
+        name = ("xa", "xb")[k % 2]
+        ids = [DstId(rid=topo.addr(c)[0], pnc=topo.addr(c)[1]) for c in peers]
+        dsts = [T[name][:, V + d * GH:V + (d + 1) * GH] for d in range(N - 1)]
+        emit("g", lambda: g.remote_dma_fused([RemoteDMATransfer(dst_ids=ids, dma_engine_mask=mask, remote_sem=T.sem["ar%d" % k],
+                                                                src=T[name][:, 0:GH], dsts=dsts)], local_sem=T.sem["lo%d" % k]),
+             [(name, 0, GH, None)], [], "r", "lo%d" % k, neng)
+        emit("x", None, [], [(name, V, W, None)], "a", "ar%d" % k, neng * (N - 1))
+
+    def col(k):
+        return ap("col", k, k + 1)
+
+    def bmat(k, j, p=128):
+        return ap("bs", 144 * k + 15 - j, 144 * k + 143 - j, p=p)
+
+    def ident(k):
+        return ap("ids", 128 * k, 128 * k + 128)
+
+    def mat(k, p=128):
+        return ap("ms", 128 * k, 128 * k + 128, p=p)
+
+    B1, BH, BF, BO2, BO3, B8 = range(6)
+    I1, INEG, I4096, IBIG, I304, I16TH, I4864, I16, IHUGE = range(9)
+    ONES, TRI, A1, ALL, E8, MGE, MLE, MTMP = range(8)
+    P, PM, C0, C15, G0, G15, WF, WA, WB, WO2, WC, WO3, JJ, NB = range(14)
+
+    def jf(k, c0=0, c1=273, step=1):
+        return ap("jf", 288 * k + c0, 288 * k + c1, step, p=8)
+    LM, NE, N2, THR, TNEG, TPOS, NLM = range(7)
+
+    dmas("y", load("xa", 0, "x0", 0, GH))
+    dmas("s", load("sgi", 0, "sg", 0, 273, 1) + load("lmi", 0, "lm", 0, 273, 1))
+    dmas("y", load("adi", 0, "ad", 0, 256))
+    dmas("y", load("xa", GH, "x0", GH, V // 2))
+    dmas("y", load("xa", V // 2, "x0", V // 2, V))
+    iota(ap("ic"), [[1, 144]], 0, 0)
+    iota(ap("pi", 0, 1), [[1, 1]], 0, 1)
+    iota(ap("col", G0, G15 + 1), [[15, 2]], 0, 16)
+    iota(ap("c16"), [[0, 16], [1, 16]], 0, 0)
+    iota(ap("pt", 256, LW), [[16, 48]], 2048, 0)
+    exchange(0)
+    iota(ap("k16"), [[16, 256]], 0, 0)
+    iota(ap("mw", 3 * W // 2, 2 * W), [[0, W // 2]], 0, 0)
+    fill(ap("mw", 0, W // 2), 0.0)
+    cp(col(P), ap("pi", 0, 1))
+    ts(ap("pi", 1, 2), ap("pi", 0, 1), 15, A.bitwise_and)
+    cp(ap("icf"), ap("ic", 0, 16))
+    ts(ident(I1), ap("ic", 0, 128), col(P), A.is_equal)
+    cp(col(PM), ap("pi", 1, 2))
+    act(ap("mw", W // 2, W), ap("mw", 0, W // 2), F.Copy)
+    for k, w in ((INEG, -1.0), (I304, float(LW)), (I16TH, 0.0625), (I4096, float(V)), (I4864, float(W)), (I16, 16.0), (IHUGE, -131072.0)):
+        act(ident(k), ident(I1), F.Copy, scale=w)
+    act(ap("mw", W, 3 * W // 2), ap("mw", 0, W // 2), F.Copy)
+    act(ap("xo", 0, V // 2), ap("xa", 0, V // 2), F.Copy)
+    for k in range(8):
+        fill(ap("bt", LW * k + 256, LW * k + LW), 0.0)
+    fill(mat(ALL), 1.0)
+    fill(col(NB), -16.5)
+    tt(col(C0), col(P), col(PM), A.subtract)
+    ts(ap("oh"), ap("icf"), col(PM), A.is_equal)
+    cp(ap("ofc"), ap("icf"))
+    ts(col(JJ), col(PM), -7.5, A.add)
+    ts(col(C15), col(C0), 15.0, A.add)
+
+    def oh(k):
+        return ap("oh", k, k + 1)
+    ts(col(WF), oh(3), oh(4), A.add, -2 * BIG, A.mult)
+    ts(col(WA), oh(2), -BIG, A.mult, oh(0), A.add)
+    ts(col(WB), oh(6), 0.0625, A.mult, oh(1), A.add)
+    ts(col(WC), oh(2), oh(5), A.add)
+    emit("v", lambda: g.vector.tensor_reduce(col(WO3)[0], T.oh[:, 7:11], AxisListType.X, A.add), [("oh", 7, 11, None)], col(WO3)[1])
+    cp(ap("of1"), ap("adi"))
+    ts(ap("s0"), ap("adi"), -S0, A.add)
+    ts(ap("bs", 0, 144), ap("ic"), col(C15), A.is_equal)
+    ts(ap("bs", 144 * BH, 144 * BH + 144), ap("ic"), col(C15), A.is_equal, 0.5, A.mult)
+    ts(ap("bs", 144 * B8, 144 * B8 + 144), ap("ic"), col(G15), A.is_equal)
+    ts(mat(MGE), ap("ic", 0, 128), col(G0), A.is_ge)
+    ts(mat(MLE), ap("ic", 0, 128), col(G15), A.is_le)
+    ts(col(WO2), col(WA), col(WB), A.add, col(WF), A.add)
+    tt(col(WO3), col(WO3), col(WC), A.add)
+    ts(ap("pt", 0, 256), ap("s0"), MAGIC, A.add, MAGIC, A.subtract)
+    tt(mat(E8), mat(MGE), mat(MLE), A.mult)
+    ts(jf(LM), ap("lmi", 0, 273, p=8), 0.0, A.add)
+    ts(jf(NE), ap("sgi", 0, 273, p=8), 1.0, A.not_equal, 99.0, A.mult)
+    ts(jf(N2), ap("sgi", 0, 273, p=8), 2.0, A.not_equal)
+    tt(ap("pj", 0, 256), ap("s0"), ap("pt", 0, 256), A.subtract)
+    tt(jf(THR), jf(LM), jf(N2), A.mult)
+    ts(mat(MGE), ap("ic", 0, 128), col(C0), A.is_ge)
+    ts(mat(MLE), ap("ic", 0, 128), col(C15), A.is_le, -1.0, A.mult)
+    act(jf(NLM, 256, 272), jf(LM, 256, 272), F.Copy, scale=-1.0)
+    ts(col(WA), col(PM), float(GH), A.add)
+    act(ap("v0", 0, 16), ap("icf"), F.Identity, bias=col(WA), scale=16.0)
+    ts(mat(MTMP), ap("ic", 0, 128), col(P), A.is_ge)
+    ts(jf(TNEG, 256, 272), jf(THR, 256, 272), -1.0 / 32, A.mult, -1.0 / 64, A.add)
+    ts(jf(TPOS, 0, 256), jf(THR, 0, 256), 1.0 / 32, A.mult, 1.0 / 64, A.add)
+    tt(mat(ONES), mat(MGE), mat(MLE), A.mult)
+    tt(mat(TRI), mat(MTMP), mat(MLE), A.mult)
+    dmas("y", [(o, i, [("xa", GH, V, None)], wr) for o, i, rd, wr in load("w2", 0, "xi", 0, GH) + load("w2", GH + V, "xi", 0, V)])
+    mm(ap("p0", 0, 256), mat(E8, 8), jf(NE, 0, 256), True, True)
+    for i in range(16):
+        mm(ap("p1", 0, 16), bmat(B8, i, 8), jf(LM, i, 256, 16), i == 0, i == 15)
+    mm(ap("p1", 16, 32), mat(E8, 8), jf(NE, 256, 272), True, True)
+    mm(ap("p1", 32, 48), mat(E8, 8), jf(TNEG, 256, 272), True, True)
+    mm(ap("p1", 48, 64), mat(E8, 8), jf(NLM, 256, 272), True, True)
+    mm(ap("p1", 64, 65), mat(E8, 8), jf(THR, 272, 273), True, True)
+    mm(ap("p1", 65, 66), mat(E8, 8), jf(LM, 272, 273), True, True)
+    mm(ap("p1", 66, 67), mat(E8, 8), jf(NE, 272, 273), True, True)
+    mm(ap("p3", 0, 256), ident(I304), ap("pj", 0, 256), True, False)
+    mm(ap("p3", 0, 256), ident(I16TH), ap("pt", 0, 256), False, True)
+    act(mat(MTMP), mat(ONES), F.Copy, scale=1.0 / 32)
+    ts(ap("dia"), ap("c16"), col(PM), A.is_equal)
+    for k, w in ((BO2, WO2), (BO3, WO3)):
+        ts(ap("bs", 144 * k, 144 * k + 144), ap("ic"), col(C15), A.is_equal, col(w), A.mult)
+    tt(mat(A1), mat(MTMP), ident(INEG), A.add)
+    for k in range(3):
+        act(ap("pj", LW * k + 256, LW * k + LW), ap("ic", 0, 48), F.Identity, bias=col(JJ), scale=0.0)
+    for k in (1, 2):
+        act(ap("pt", LW * k + 256, LW * k + LW), ap("pt", 256, LW), F.Copy)
+    fill(ap("bt", 7 * LW, 7 * LW + 256), 1.0)
+    act(ap("th", 0, 67), ap("p1", 0, 67), F.Copy)
+    act(ap("t9"), ap("p0", 0, 256), F.Copy)
+    ts(ap("of2"), ap("p3", 0, 256), 2408.0, A.add)
+    tt(ap("th", 16, 32), ap("th", 16, 32), ap("th", 0, 16), A.add)
+    ts(ap("m13"), ap("icf"), 0.0, A.mult, ap("th", 66, 67), A.is_equal)
+    dmas("y", torow("pj", 0, 0, (0, 1)) + torow("pt", 0, 1, (0, 1)) + torow("bt", 7 * LW, 5, (0, 1)))
+
+    for t in range(1, STEPS + 1):
+        cur, nxt = ("xa", "xb")[(t - 1) % 2], ("xa", "xb")[t % 2]
+        names, last = t > 1, t == STEPS
+        order = ORDER[1 if t == 1 else 0].split()
+        cmps = [c for c in range(4) if "C%d" % (2 * c) in order or "P%d" % c in order]
+        slot = 1 + (t % 2)
+        b = ap("bt", LW * (t - 1), LW * (t - 1) + 256)
+
+        free, held = list(BANKS), {}
+
+        def gather(q, o, i):
+            if q == "v":
+                cp(o, i)
+            else:
+                act(o, i, F.Copy)
+
+        def g1(q, c):
+            gather(q, ap("dd", 1024 * c, 1024 * c + 1024), ind(ap(cur), ap("of1", 64 * c, 64 * c + 64)))
+
+        def g2(q, c):
+            gather(q, ap("go", 1024 * c, 1024 * c + 1024), ind(ap("mw"), ap("of2", 64 * c, 64 * c + 64)))
+
+        def own(q, c):
+            o, i = ap("xo", 1024 * c, 1024 * c + 1024), ap(cur, 1024 * c, 1024 * c + 1024)
+            if t == 1 and c < 2:
+                return
+            if c in OWN_DMA and names:
+                dmas("y", [(o[0], i[0], i[1], o[1])])
+            else:
+                gather(q, o, i)
+
+        def fused(c):
+            tt(ap("dd", 1024 * c, 1024 * c + 1024), ind(ap(cur), ap("of1", 64 * c, 64 * c + 64)), ap("xo", 1024 * c, 1024 * c + 1024), A.subtract)
+
+        def cmpf(q, c):
+            o, i = ap("cm", 1024 * c, 1024 * c + 1024), ap("dd", 1024 * c, 1024 * c + 1024)
+            if q == "s":
+                act(o, i, F.Sign, bias=col(NB), scale=-1.0)
+            else:
+                ts(o, i, -16.5, A.is_lt, 0.5, A.subtract)
+
+        def relu(q, k):
+            o = ap("w2", GH + 512 * k, GH + 512 * k + 512) if "A%d" % (k // 2) in order else ap("rr", 512 * k, 512 * k + 512)
+            i = ap("dd", 512 * k, 512 * k + 512)
+            if q == "s":
+                act(o, i, F.Relu)
+            else:
+                ts(o, i, 0.0, A.max)
+
+        def adddma(c):
+            o, i = ap("w2", GH + 1024 * c, GH + 1024 * c + 1024), ap(cur, 1024 * c, 1024 * c + 1024)
+            sem = "dm%d" % nd[0]
+            nd[0] += 1
+            emit("g", lambda: g.dma_start(o[0], i[0], accum_op=A.add), i[1] + o[1], o[1], "d", sem, 16)
+
+        def ypsum(k):
+            held["y", k] = free.pop(0)
+            mm(ap("p%d" % held["y", k]), ident(I1), ap("dd", 512 * k, 512 * k + 512), True, "e%d" % k not in order)
+
+        def mx(k):
+            tt(ap("w2", GH + 512 * k, GH + 512 * k + 512), ap("p%d" % held["y", k]), ap(cur, 512 * k, 512 * k + 512), A.max)
+            if "e%d" % k not in order:
+                free.append(held["y", k])
+
+        def dpsum(k):
+            held["d", k] = free.pop(0)
+            mm(ap("p%d" % held["d", k]), ident(INEG), ap(cur, 512 * k, 512 * k + 512), True, False)
+            mm(ap("p%d" % held["d", k]), ident(I1), ap("dd", 512 * k, 512 * k + 512), False, True)
+
+        def dafter(k):
+            held["d", k] = held["y", k]
+            mm(ap("p%d" % held["d", k]), ident(INEG), ap(cur, 512 * k, 512 * k + 512), False, True)
+
+        def cmp_(q, k):
+            o, i = ap("cm", 512 * k, 512 * k + 512), ap("p%d" % held["d", k])
+            if q == "s":
+                act(o, i, F.Sign, bias=col(NB), scale=-1.0)
+            else:
+                ts(o, i, -16.5, A.is_lt, 0.5, A.subtract)
+            if "R%d" % k not in order or "D%d" % k in order:
+                free.append(held["d", k])
+
+        def rise(k):
+            act(ap("rr", 512 * k, 512 * k + 512), ap("p%d" % held["d", k]), F.Relu)
+            free.append(held["d", k])
+
+        def addx(k):
+            held["y", k] = free.pop(0)
+            mm(ap("p%d" % held["y", k]), ident(I1), ap(cur, 512 * k, 512 * k + 512), True, False)
+            mm(ap("p%d" % held["y", k]), ident(I1), ap("rr", 512 * k, 512 * k + 512), False, True)
+
+        def mxs(k):
+            act(ap("w2", GH + 512 * k, GH + 512 * k + 512), ap("p%d" % held["y", k]), F.Copy)
+            free.append(held["y", k])
+
+        def pick(out, k, src, c, start, stop):
+            for j in range(16):
+                mm(out, bmat(k, j), ap(src, 1024 * c + j, 1024 * c + 1024, 16), start and j == 0, stop and j == 15)
+
+        def void(c):
+            ts(ap("rw", 64 * c, 64 * c + 64), ap("p3", 64 * c, 64 * c + 64), -1.5 * BIG, A.is_lt, 9.0, A.mult)
+
+        def count(c):
+            o = ap("p%d" % (c % 2), 0, 64)
+            pick(o, BH if c in cmps else B1, "cm", c, True, not names)
+            if names:
+                mm(o, ident(I1), ap("rw", 64 * c, 64 * c + 64), False, True)
+
+        def nexts(c):
+            if names:
+                o = ap("p3", 64 * c, 64 * c + 64)
+                mm(o, ident(INEG), ap("pt", 64 * c, 64 * c + 64), True, False)
+                mm(o, ident(INEG), ap("pj", 64 * c, 64 * c + 64), False, False)
+                pick(o, BO2, "go", c, False, True)
+            if t == 5:
+                pick(ap("p4", 64 * c, 64 * c + 64), BO3, "go", c, True, True)
+            if t == 6:
+                pick(ap("p4", 64 * c, 64 * c + 64), BO3, "go", c, False, False)
+
+        def crash(c):
+            o = ap("p%d" % (c % 2), 0, 64)
+            ts(ap("cr", 64 * c, 64 * c + 64), o, 0.5, A.is_gt)
+            tt(ap("cr1", 64 * c, 64 * c + 64), o, ap("t9", 64 * c, 64 * c + 64), A.is_gt)
+
+        def sel(q, c0, c1):
+            gather(q, ap(nxt, c0, c1), ind(ap("w2", GH), ap("idx", c0 // 16, c1 // 16)))
+
+        def update():
+            items = []
+            if 3 <= t <= 5:
+                items += torow("pj", LW * (3 - slot), 0, (0, 1)) + torow("pt", LW * (3 - slot), 1, (0, 1))
+            if t <= 5:
+                items += torow("bt", LW * (t - 2), 5 + t, (0, 1))
+                dmas("y", items)
+
+        if last:
+            mm(ap("p4", 0, 256), ident(I16), ap("pt", LW * (3 - slot), LW * (3 - slot) + 256), True, False)
+            mm(ap("p4", 0, 256), ident(I16), ap("pj", LW * (3 - slot), LW * (3 - slot) + 256), False, False)
+
+        def j1():
+            for i in range(16):
+                mm(ap("p1", 0, 16), bmat(B1, i), ap("cr", i, 256, 16), i == 0, i == 15)
+
+        def q0():
+            mm(ap("p2", 0, 256), mat(E8, 8), jf(TPOS, 0, 256), True, False)
+
+        def q1():
+            mm(ap("p2", 0, 256), mat(A1), ap("cr"), False, False)
+            mm(ap("p2", 0, 256), mat(TRI), ap("cr1"), False, False)
+            mm(ap("p0", 0, 256), ident(I1), ap("k16"), True, False)
+
+        def j2():
+            tt(ap("d1", 0, 16), ap("p1", 0, 16), ap("th", 0, 16), A.is_gt)
+            tt(ap("d1", 16, 32), ap("p1", 0, 16), ap("th", 16, 32), A.is_gt)
+            mm(ap("p1", 32, 48), mat(A1), ap("d1", 0, 16), True, False)
+            mm(ap("p1", 32, 48), mat(TRI), ap("d1", 16, 32), False, True)
+            mm(ap("p1", 48, 64), mat(ONES), ap("d1", 0, 16), True, True)
+
+        def j3():
+            tt(ap("bd"), ap("p1", 32, 64), ap("th", 32, 64), A.is_lt)
+            emit("v", lambda: g.vector.tensor_reduce(T.n3[:, 0:1], T.bd[:, 16:32], AxisListType.X, A.add), ap("bd", 16, 32)[1], ap("n3")[1])
+            emit("v", lambda: g.vector.tensor_tensor_scan(T.w3[:, 0:16], T.m13[:, 0:16], T.bd[:, 16:32], 0.0, A.mult, A.add),
+                 reg(ap("m13"), ap("bd", 16, 32)), ap("w3")[1])
+            ts(ap("ed", 0, 2), ap("th", 64, 66), ap("n3", 0, 1), A.is_lt)
+            tt(ap("rs"), ap("bd", 0, 16), ap("w3"), A.add)
+            mm(ap("p1", 64, 65), mat(ALL), ap("ed", 1, 2), True, True)
+            tt(ap("rex"), ind(ap("rs"), ap("ofc")), ap("dia"), A.mult)
+            mm(ap("p2", 0, 256), mat(ONES), ap("rex"), False, True)
+
+        def j4():
+            ts(ap("sc", 0, 1), ap("p1", 64, 65), 63.5, A.is_gt, ap("ed", 0, 1), A.add)
+            if not last:
+                ts(ap("v0", 16, 32), ap("p2", 0, 16), ap("sc", 0, 1), A.is_lt, -float(GH), A.mult)
+                tt(ap("v0", 32, 48), ap("v0", 16, 32), ap("v0", 0, 16), A.add)
+                cp(ap("ix0"), ap("v0", 32, 48))
+                act(ap(nxt, 0, GH), ind(ap("w2", 0, 2 * GH), ap("ix0")), F.Copy)
+                exchange(t)
+
+        def c5():
+            if t == 5:
+                act(ap("bt", 6 * LW, 6 * LW + 256), ap("p4", 0, 256), F.Copy)
+                dmas("y", torow("bt", 6 * LW, 6, (0, 1)))
+        calls = {"y": void, "n": count, "x": nexts, "k": crash, "m": mx, "a": ypsum, "d": dpsum, "e": dafter,
+                 "D": dpsum, "R": rise, "b": addx, "M": mxs, "F": fused, "A": adddma,
+                 "j1": j1, "j2": j2, "j3": j3, "j4": j4, "q0": q0, "q1": q1, "u5": c5, "up": update}
+        either = {"g": g1, "h": g2, "c": cmp_, "p": cmpf, "l": relu, "z": own}
+        for w in order:
+            if w in calls:
+                calls[w]()
+            elif w[0] in calls:
+                calls[w[0]](int(w[1:]))
+            else:
+                either[w[0].lower()]("v" if w[0].islower() else "s", int(w[1:]))
+        ts(b, ap("p2", 0, 256), ap("sc", 0, 1), A.is_lt)
+        mm(ap("p0", 0, 256), ident(I4096), b, False, True)
+        if names:
+            ts(ap("rw"), b, BIG, A.mult, -BIG / 2, A.add)
+        if not last:
+            dmas("y", torow("bt", LW * (t - 1), 2, (0,)) + torow("bt", LW * (t - 1), 3 + t % 2, (1,)))
+        ts(ap("idx"), ap("p0", 0, 256), col(PM), A.add)
+
+        def address():
+            tt(ap("nbe"), ap("p3", 0, 256), ap("rw"), A.is_gt)
+            tt(ap("p3", 256, 512), ap("p3", 0, 256), ap("nbe"), A.mult)
+            tt(ap("p3", 0, 256), ap("p3", 256, 512), ap("s0"), A.add)
+        if not last:
+            sv = SEL_V if names else SEL_V_FIRST
+            cuts = [sv] + [c for c in (1024, 2048, 3072, 4096) if c > sv + 256]
+            for c0, c1 in zip(cuts, cuts[1:]):
+                sel("s", c0, c1)
+            if names:
+                address()
+                s = ap("p3", 0, 256)
+                pt, pj = ap("pt", LW * slot, LW * slot + 256), ap("pj", LW * slot, LW * slot + 256)
+                ts(pt, s, MAGIC, A.add, MAGIC, A.subtract)
+                ts(ap("of1"), s, S0, A.add)
+                tt(pj, s, pt, A.subtract)
+                mm(ap("p1", 0, 256), ident(I4864), ap("nbe"), True, False)
+                mm(ap("p1", 0, 256), ident(I16TH), pt, False, False)
+                mm(ap("p1", 0, 256), ident(I304), pj, False, True)
+                sel("v", GH, (GH + sv) // 2)
+                ts(ap("of2"), ap("p1", 0, 256), 2408.0, A.add)
+                sel("v", (GH + sv) // 2, sv)
+            else:
+                sel("v", GH, sv)
+        else:
+            mm(ap("p4", 0, 256), ident(IHUGE), b, False, True)
+            for k in range(STEPS):
+                mm(ap("p5", 0, 256), ident(I1), ap("bt", LW * k, LW * k + 256), k == 0, k == STEPS - 1)
+            ts(ap("ou"), ap("p4", 0, 256), 16 * S0, A.add, -1.0, A.max)
+            dmas("y", store("yu", "ou", 0, 256))
+            for k, (c0, c1) in enumerate(zip(LAST_CUTS, LAST_CUTS[1:])):
+                sel("sv"[k % 2], c0, c1)
+                dmas("y", store("yx", nxt, c0, c1))
+                if k == 0:
+                    act(ap("oi"), ap("p5", 0, 256), F.Identity, bias=1.0)
+                    dmas("y", store("yi", "oi", 0, 256))
+                if k == 3:
+                    address()
+                    ts(ap("oa"), ap("p3", 0, 256), 16.0, A.mult, 16 * S0, A.add)
+            dmas("y", store("ya", "oa", 0, 256))
+
+    def meet(a, c):
+        return a[0] == c[0] and a[1] < c[2] and c[1] < a[2] and (a[3] is None or c[3] is None or a[3] == c[3])
+
+    hist = {}
+    for i, o in enumerate(ops):
+        deps = set()
+        for rw, regs in (("r", o["rd"]), ("w", o["wr"])):
+            for r in regs:
+                psum = r[0][0] == "p" and r[0][1].isdigit()
+                for (j, rw2, r2) in hist.get(r[0], []):
+                    p = ops[j]
+                    if j == i or not meet(r, r2):
+                        continue
+                    same = p["q"] == o["q"] and p["kind"] == "c" and o["kind"] == "c"
+                    if rw == "r" and rw2 == "r" and (same or not psum):
+                        continue
+                    if same and o["q"] == "t":
+                        continue
+                    if p["kind"] == "d" and o["kind"] == "d" and p["sem"] == o["sem"]:
+                        continue
+                    deps.add(j)
+        o["deps"] = deps if o["kind"] != "a" else set()
+        for rw, regs in (("r", o["rd"]), ("w", o["wr"])):
+            for r in regs:
+                h = hist.setdefault(r[0], [])
+                if rw == "w" and r[3] is None:
+                    h[:] = [e for e in h if not (e[2][1] >= r[1] and e[2][2] <= r[2])]
+                h.append((i, rw, r))
+    for o in ops:
+        top = {}
+        for j in o["deps"]:
+            p = ops[j]
+            k = p["q"] if p["kind"] == "c" else p["sem"]
+            top[k] = max(top.get(k, -1), j)
+        o["deps"] = sorted(top.values())
+    known = {q: {} for q in Q}
+    for i, o in enumerate(ops):
+        if o["kind"] == "a":
+            o["clock"] = {}
+            continue
+        kn = known[o["q"]]
+        keep = []
+        for j in reversed(o["deps"]):
+            p = ops[j]
+            k = p["q"] if p["kind"] == "c" else p["sem"]
+            if kn.get(k, -1) >= (j if p["kind"] == "c" else 0):
+                continue
+            keep.append(j)
+            p["need"] = True
+            kn[k] = j if p["kind"] == "c" else 0
+            for k2, v2 in p["clock"].items():
+                kn[k2] = max(kn.get(k2, -1), v2)
+        o["deps"] = keep
+        o["clock"] = dict(kn) if o["kind"] == "c" else {}
+    count_ = {q: 0 for q in Q}
+    waited = {}
+    total = {}
+    for o in ops:
+        if o["kind"] != "c":
+            total[o["sem"]] = o["n"]
+        if o["kind"] == "a":
+            continue
+        for j in o["deps"]:
+            p = ops[j]
+            s, n = ("q" + p["q"], p["at"]) if p["kind"] == "c" else (p["sem"], p["n"])
+            Q[o["q"]].wait_ge(T.sem[s], n)
+            waited[s] = max(waited.get(s, 0), n)
+        r = o["fn"]()
+        if o["kind"] == "d":
+            r.then_inc(T.sem[o["sem"]], 16)
+        elif o["kind"] == "c" and o["need"]:
+            count_[o["q"]] += 1
+            o["at"] = count_[o["q"]]
+            r.then_inc(T.sem["q" + o["q"]], 1)
+    for s in total:
+        if waited.get(s, 0) < total[s]:
+            g.wait_ge(T.sem[s], total[s])

@@ -40,14 +40,14 @@ for _k in range(8):
 NDMA = 80
 SEMAPHORES = ["qv", "qs", "qt", "qg"] + ["dm%d" % k for k in range(NDMA)] + ["ar%d" % k for k in range(STEPS)] + ["lo%d" % k for k in range(STEPS)]
 
-SEL_V = 1920
+SEL_V = 896
 SEL_V_FIRST = 2304
 LAST_CUTS = (0, 512, 1280, 2176, 3072, 4096)
 BANKS = (5, 6, 7)
-OWN_DMA = ()
+OWN_DMA = (0, 1, 2)
 ORDER = {
-    0: "H2 h3 h1 q0 H0 G1 x2 z2 z0 x3 G3 x0 x1 d3 d2 C3 F0 d6 y1 y0 C2 d7 a7 P0 y3 C6 n1 F2 up k1 p2 n0 a2 C7 y2 L4 k0 u5 L1 n3 m2 L0 k3 n2 L5 a3 k2 m3 a6 j1 m7 b0 q1 j2 m6 b5 M0 b4 M5 M4 j3 b1 M1 j4",
-    1: "z0 q0 F0 G2 z1 p0 G3 d4 d5 n0 C4 F1 C5 d6 p1 l1 k0 d7 C6 n1 n2 b1 C7 k1 n3 k2 l0 b0 l2 k3 M0 a4 j1 m4 a5 M1 b2 l3 m5 M2 a6 q1 j2 a7 m6 b3 j3 j4 m7 M3",
+    0: "z0 z1 z2 h3 H2 h0 x3 F0 q0 H1 x2 x0 x1 F1 G3 l1 P1 L0 y2 y1 a7 y3 d6 d7 n1 p0 C6 y0 F2 k1 C7 L3 L2 A0 n0 A1 p2 n3 k0 n2 m7 k3 k2 a6 m6 j1 u5 q1 L5 j2 l4 b5 j3 up b4 M5 j4 M4",
+    1: "z0 q0 z1 G2 F0 G3 L0 p0 F1 d4 l1 d5 C4 L2 n0 k0 p1 C5 A0 l3 d6 d7 n1 k1 a4 C7 m4 n2 A1 k2 C6 n3 k3 a6 a5 j1 q1 m6 a7 j2 m5 j3 m7 j4",
 }
 
 
@@ -174,11 +174,12 @@ def rank_program(g, core, T, topo):
     iota(ap("ic"), [[1, 144]], 0, 0)
     iota(ap("pi", 0, 1), [[1, 1]], 0, 1)
     iota(ap("col", G0, G15 + 1), [[15, 2]], 0, 16)
-    iota(ap("c16"), [[0, 16], [1, 16]], 0, 0)
+    iota(mat(MGE), [[16, 8], [0, 16]], 0, 0)
     iota(ap("pt", 256, LW), [[16, 48]], 2048, 0)
     exchange(0)
+    iota(ap("c16"), [[0, 16], [1, 16]], 0, 0)
     iota(ap("k16"), [[16, 256]], 0, 0)
-    iota(ap("mw", 3 * W // 2, 2 * W), [[0, W // 2]], 0, 0)
+    iota(ap("mw", W, 2 * W), [[0, W]], 0, 0)
     fill(ap("mw", 0, W // 2), 0.0)
     cp(col(P), ap("pi", 0, 1))
     ts(ap("pi", 1, 2), ap("pi", 0, 1), 15, A.bitwise_and)
@@ -188,11 +189,11 @@ def rank_program(g, core, T, topo):
     act(ap("mw", W // 2, W), ap("mw", 0, W // 2), F.Copy)
     for k, w in ((INEG, -1.0), (I304, float(LW)), (I16TH, 0.0625), (I4096, float(V)), (I4864, float(W)), (I16, 16.0), (IHUGE, -131072.0)):
         act(ident(k), ident(I1), F.Copy, scale=w)
-    act(ap("mw", W, 3 * W // 2), ap("mw", 0, W // 2), F.Copy)
-    act(ap("xo", 0, V // 2), ap("xa", 0, V // 2), F.Copy)
     for k in range(8):
-        fill(ap("bt", LW * k + 256, LW * k + LW), 0.0)
-    fill(mat(ALL), 1.0)
+        act(ap("bt", LW * k + 256, LW * k + LW), ap("mw", 0, 48), F.Copy)
+    act(mat(ALL), ap("mw", 0, 128), F.Identity, bias=1.0)
+    act(ap("bt", 7 * LW, 7 * LW + 256), ap("mw", 0, 256), F.Identity, bias=1.0)
+    act(ap("xo", 0, V // 2), ap("xa", 0, V // 2), F.Copy)
     fill(col(NB), -16.5)
     tt(col(C0), col(P), col(PM), A.subtract)
     ts(ap("oh"), ap("icf"), col(PM), A.is_equal)
@@ -212,27 +213,24 @@ def rank_program(g, core, T, topo):
     ts(ap("bs", 0, 144), ap("ic"), col(C15), A.is_equal)
     ts(ap("bs", 144 * BH, 144 * BH + 144), ap("ic"), col(C15), A.is_equal, 0.5, A.mult)
     ts(ap("bs", 144 * B8, 144 * B8 + 144), ap("ic"), col(G15), A.is_equal)
-    ts(mat(MGE), ap("ic", 0, 128), col(G0), A.is_ge)
-    ts(mat(MLE), ap("ic", 0, 128), col(G15), A.is_le)
+    ts(mat(E8), mat(MGE), col(G0), A.is_equal)
+    ts(mat(ONES), mat(MGE), col(C0), A.is_equal, -1.0, A.mult)
+    ts(mat(MTMP), mat(MGE), col(C0), A.is_equal, -1.0 / 32, A.mult)
     ts(col(WO2), col(WA), col(WB), A.add, col(WF), A.add)
     tt(col(WO3), col(WO3), col(WC), A.add)
     ts(ap("pt", 0, 256), ap("s0"), MAGIC, A.add, MAGIC, A.subtract)
-    tt(mat(E8), mat(MGE), mat(MLE), A.mult)
     ts(jf(LM), ap("lmi", 0, 273, p=8), 0.0, A.add)
     ts(jf(NE), ap("sgi", 0, 273, p=8), 1.0, A.not_equal, 99.0, A.mult)
     ts(jf(N2), ap("sgi", 0, 273, p=8), 2.0, A.not_equal)
     tt(ap("pj", 0, 256), ap("s0"), ap("pt", 0, 256), A.subtract)
     tt(jf(THR), jf(LM), jf(N2), A.mult)
-    ts(mat(MGE), ap("ic", 0, 128), col(C0), A.is_ge)
-    ts(mat(MLE), ap("ic", 0, 128), col(C15), A.is_le, -1.0, A.mult)
     act(jf(NLM, 256, 272), jf(LM, 256, 272), F.Copy, scale=-1.0)
     ts(col(WA), col(PM), float(GH), A.add)
     act(ap("v0", 0, 16), ap("icf"), F.Identity, bias=col(WA), scale=16.0)
-    ts(mat(MTMP), ap("ic", 0, 128), col(P), A.is_ge)
+    ts(mat(MLE), ap("ic", 0, 128), col(P), A.is_ge)
     ts(jf(TNEG, 256, 272), jf(THR, 256, 272), -1.0 / 32, A.mult, -1.0 / 64, A.add)
     ts(jf(TPOS, 0, 256), jf(THR, 0, 256), 1.0 / 32, A.mult, 1.0 / 64, A.add)
-    tt(mat(ONES), mat(MGE), mat(MLE), A.mult)
-    tt(mat(TRI), mat(MTMP), mat(MLE), A.mult)
+    tt(mat(TRI), mat(ONES), mat(MLE), A.mult)
     dmas("y", [(o, i, [("xa", GH, V, None)], wr) for o, i, rd, wr in load("w2", 0, "xi", 0, GH) + load("w2", GH + V, "xi", 0, V)])
     mm(ap("p0", 0, 256), mat(E8, 8), jf(NE, 0, 256), True, True)
     for i in range(16):
@@ -245,7 +243,6 @@ def rank_program(g, core, T, topo):
     mm(ap("p1", 66, 67), mat(E8, 8), jf(NE, 272, 273), True, True)
     mm(ap("p3", 0, 256), ident(I304), ap("pj", 0, 256), True, False)
     mm(ap("p3", 0, 256), ident(I16TH), ap("pt", 0, 256), False, True)
-    act(mat(MTMP), mat(ONES), F.Copy, scale=1.0 / 32)
     ts(ap("dia"), ap("c16"), col(PM), A.is_equal)
     for k, w in ((BO2, WO2), (BO3, WO3)):
         ts(ap("bs", 144 * k, 144 * k + 144), ap("ic"), col(C15), A.is_equal, col(w), A.mult)
@@ -254,7 +251,6 @@ def rank_program(g, core, T, topo):
         act(ap("pj", LW * k + 256, LW * k + LW), ap("ic", 0, 48), F.Identity, bias=col(JJ), scale=0.0)
     for k in (1, 2):
         act(ap("pt", LW * k + 256, LW * k + LW), ap("pt", 256, LW), F.Copy)
-    fill(ap("bt", 7 * LW, 7 * LW + 256), 1.0)
     act(ap("th", 0, 67), ap("p1", 0, 67), F.Copy)
     act(ap("t9"), ap("p0", 0, 256), F.Copy)
     ts(ap("of2"), ap("p3", 0, 256), 2408.0, A.add)
@@ -345,7 +341,8 @@ def rank_program(g, core, T, topo):
                 free.append(held["d", k])
 
         def rise(k):
-            act(ap("rr", 512 * k, 512 * k + 512), ap("p%d" % held["d", k]), F.Relu)
+            o = ap("w2", GH + 512 * k, GH + 512 * k + 512) if "A%d" % (k // 2) in order else ap("rr", 512 * k, 512 * k + 512)
+            act(o, ap("p%d" % held["d", k]), F.Relu)
             free.append(held["d", k])
 
         def addx(k):
@@ -457,19 +454,23 @@ def rank_program(g, core, T, topo):
                 either[w[0].lower()]("v" if w[0].islower() else "s", int(w[1:]))
         ts(b, ap("p2", 0, 256), ap("sc", 0, 1), A.is_lt)
         mm(ap("p0", 0, 256), ident(I4096), b, False, True)
-        if names:
+        if names and not last:
             ts(ap("rw"), b, BIG, A.mult, -BIG / 2, A.add)
+            tt(ap("nbe"), ap("p3", 0, 256), ap("rw"), A.is_gt)
         if not last:
             dmas("y", torow("bt", LW * (t - 1), 2, (0,)) + torow("bt", LW * (t - 1), 3 + t % 2, (1,)))
         ts(ap("idx"), ap("p0", 0, 256), col(PM), A.add)
 
         def address():
-            tt(ap("nbe"), ap("p3", 0, 256), ap("rw"), A.is_gt)
+            if last:
+                ts(ap("rw"), b, BIG, A.mult, -BIG / 2, A.add)
+                tt(ap("nbe"), ap("p3", 0, 256), ap("rw"), A.is_gt)
             tt(ap("p3", 256, 512), ap("p3", 0, 256), ap("nbe"), A.mult)
             tt(ap("p3", 0, 256), ap("p3", 256, 512), ap("s0"), A.add)
         if not last:
             sv = SEL_V if names else SEL_V_FIRST
-            cuts = [sv] + [c for c in (1024, 2048, 3072, 4096) if c > sv + 256]
+            lo = V + GH - sv
+            cuts = [GH] + [c for c in (1024, 2048, 3072) if c < lo - 256] + [lo]
             for c0, c1 in zip(cuts, cuts[1:]):
                 sel("s", c0, c1)
             if names:
@@ -482,11 +483,11 @@ def rank_program(g, core, T, topo):
                 mm(ap("p1", 0, 256), ident(I4864), ap("nbe"), True, False)
                 mm(ap("p1", 0, 256), ident(I16TH), pt, False, False)
                 mm(ap("p1", 0, 256), ident(I304), pj, False, True)
-                sel("v", GH, (GH + sv) // 2)
+                sel("v", lo, lo + 512)
                 ts(ap("of2"), ap("p1", 0, 256), 2408.0, A.add)
-                sel("v", (GH + sv) // 2, sv)
+                sel("v", lo + 512, V)
             else:
-                sel("v", GH, sv)
+                sel("v", lo, V)
         else:
             mm(ap("p4", 0, 256), ident(IHUGE), b, False, True)
             for k in range(STEPS):

@@ -5,49 +5,46 @@ A = AluOpType
 F = ActivationFunctionType
 V, GH, W, STEPS, N = 4096, 256, 4864, 6, 4
 LW = W // 16
+CH = 1024
 BIG = 16384.0
 MAGIC = 201326592.0
 S0 = 2055.5
+U = 1.0 / 16384
 
 SCRATCH = {
     "xa": ("sbuf", [128, W], "bfloat16"), "xb": ("sbuf", [128, W], "bfloat16"),
-    "w2": ("sbuf", [128, GH + 2 * V], "bfloat16"), "mw": ("sbuf", [128, 2 * W], "bfloat16"),
+    "gw": ("sbuf", [128, 6 * CH], "bfloat16"), "gx": ("sbuf", [128, 96], "uint16"),
+    "w2": ("sbuf", [128, 3 * V], "bfloat16"), "mw": ("sbuf", [128, 2 * W], "bfloat16"),
     "dd": ("sbuf", [128, V], "bfloat16"), "cm": ("sbuf", [128, V], "bfloat16"),
     "rr": ("sbuf", [128, V], "bfloat16"), "xo": ("sbuf", [128, V], "bfloat16"), "go": ("sbuf", [128, V], "bfloat16"),
     "adi": ("sbuf", [128, 256], "int32"), "sgi": ("sbuf", [128, 288], "int32"), "lmi": ("sbuf", [128, 288], "int32"),
     "of1": ("sbuf", [128, 256], "uint16"), "of2": ("sbuf", [128, 256], "uint16"), "idx": ("sbuf", [128, 256], "uint16"),
     "ofc": ("sbuf", [128, 16], "uint16"),
-    "s0": ("sbuf", [128, 256], "float32"),
+    "s0": ("sbuf", [128, 256], "float32"), "tf": ("sbuf", [128, 256], "float32"), "i32": ("sbuf", [128, 128], "float32"),
     "pt": ("sbuf", [128, 3 * LW], "bfloat16"), "pj": ("sbuf", [128, 3 * LW], "bfloat16"),
     "bt": ("sbuf", [128, 8 * LW], "bfloat16"),
-    "cr": ("sbuf", [128, 256], "bfloat16"), "cr1": ("sbuf", [128, 256], "bfloat16"), "nbe": ("sbuf", [128, 256], "bfloat16"),
-    "t9": ("sbuf", [128, 256], "bfloat16"), "k16": ("sbuf", [128, 256], "bfloat16"), "dia": ("sbuf", [128, 256], "bfloat16"),
-    "rex": ("sbuf", [128, 256], "bfloat16"), "c16": ("sbuf", [128, 256], "bfloat16"),
+    "cr": ("sbuf", [128, 256], "bfloat16"), "nbe": ("sbuf", [128, 256], "bfloat16"), "k16": ("sbuf", [128, 256], "bfloat16"),
+    "d1": ("sbuf", [128, 256], "bfloat16"), "n2": ("sbuf", [128, 256], "bfloat16"), "zs": ("sbuf", [128, 256], "bfloat16"),
+    "seg": ("sbuf", [128, 256], "bfloat16"), "dec": ("sbuf", [128, 256], "bfloat16"), "rw": ("sbuf", [128, 256], "bfloat16"),
     "ic": ("sbuf", [128, 144], "bfloat16"), "icf": ("sbuf", [128, 16], "float32"), "pi": ("sbuf", [128, 4], "int32"),
     "col": ("sbuf", [128, 32], "float32"), "oh": ("sbuf", [128, 16], "float32"),
-    "bs": ("sbuf", [128, 6 * 144], "bfloat16"), "ids": ("sbuf", [128, 9 * 128], "bfloat16"),
-    "ms": ("sbuf", [128, 8 * 128], "bfloat16"),
-    "jf": ("sbuf", [128, 7 * 288], "bfloat16"),
-    "th": ("sbuf", [128, 96], "float32"), "m13": ("sbuf", [128, 16], "bfloat16"),
-    "d1": ("sbuf", [128, 32], "bfloat16"), "bd": ("sbuf", [128, 32], "bfloat16"), "w3": ("sbuf", [128, 16], "bfloat16"),
-    "rs": ("sbuf", [128, 16], "bfloat16"), "n3": ("sbuf", [128, 4], "float32"), "ed": ("sbuf", [128, 8], "bfloat16"),
-    "sc": ("sbuf", [128, 4], "float32"), "v0": ("sbuf", [128, 48], "float32"), "ix0": ("sbuf", [128, 16], "uint16"),
-    "rw": ("sbuf", [128, 256], "bfloat16"),
+    "bs": ("sbuf", [128, 6 * 144], "bfloat16"), "ids": ("sbuf", [128, 11 * 128], "bfloat16"),
+    "ms": ("sbuf", [128, 6 * 128], "bfloat16"),
+    "jf": ("sbuf", [128, 3 * 256], "bfloat16"), "js": ("sbuf", [128, 64], "bfloat16"), "th": ("sbuf", [128, 64], "float32"),
+    "up": ("sbuf", [128, 80], "bfloat16"), "bp": ("sbuf", [128, 256], "bfloat16"), "kq": ("sbuf", [128, 16], "bfloat16"), "ed": ("sbuf", [128, 8], "bfloat16"),
+    "sc": ("sbuf", [128, 4], "float32"), "v0": ("sbuf", [128, 32], "float32"), "ix0": ("sbuf", [128, 16], "uint16"),
     "oa": ("sbuf", [128, 256], "float32"), "ou": ("sbuf", [128, 256], "float32"), "oi": ("sbuf", [128, 256], "float32"),
 }
 for _k in range(8):
     SCRATCH["p%d" % _k] = ("psum", [128, 512], "float32")
-NDMA = 80
-SEMAPHORES = ["qv", "qs", "qt", "qg"] + ["dm%d" % k for k in range(NDMA)] + ["ar%d" % k for k in range(STEPS)] + ["lo%d" % k for k in range(STEPS)]
+NDMA = 90
+SEMAPHORES = ["qv", "qs", "qt", "qg"] + ["dm%d" % k for k in range(NDMA)] + ["ar%d" % k for k in range(2 * STEPS)] + ["lo%d" % k for k in range(2 * STEPS)]
 
-SEL_V = 896
-SEL_V_FIRST = 2304
-LAST_CUTS = (0, 512, 1280, 2176, 3072, 4096)
-BANKS = (5, 6, 7)
-OWN_DMA = (0, 1, 2)
 ORDER = {
-    0: "z0 z1 z2 h3 H2 h0 x3 F0 q0 H1 x2 x0 x1 F1 G3 l1 P1 L0 y2 y1 a7 y3 d6 d7 n1 p0 C6 y0 F2 k1 C7 L3 L2 A0 n0 A1 p2 n3 k0 n2 m7 k3 k2 a6 m6 j1 u5 q1 L5 j2 l4 b5 j3 up b4 M5 j4 M4",
-    1: "z0 q0 z1 G2 F0 G3 L0 p0 F1 d4 l1 d5 C4 L2 n0 k0 p1 C5 A0 l3 d6 d7 n1 k1 a4 C7 m4 n2 A1 k2 C6 n3 k3 a6 a5 j1 q1 m6 a7 j2 m5 j3 m7 j4",
+    1: "later G2 F0 d4 d5 X+ F1 p0 L0 C4 R4 R5 C5 L1 n0 ag n2 F3 p1 n1 w0 w2 w3 w1 A0 A2 A1 p3 n3 mg j0 k0 j1 k1 K2 K3 K4 K5 J0 I6 K6 J1 K7 J2 i7 b7 b6 up K9 S01 J5 J3 K8 M7 M6 Sac Scg s8a s14 s48 Z0 z1 Z3 h0+ h2+ x0+ H1+ H3+ x1+ x2+ x3+",
+    2: "G2 F0 up F1 p0 L0 d4 d5 C4 C5 R5 P1 R4 n0 n2 n1 ag F3 A0 A2 p3 n3 j0 mg k0 j1 k1 K2 K3 K4 K5 J0 L1 I7 I6 b7 b6 K6 J1 A1 K7 J2 K9 J3 K8 u0 u1 s14 u4 u2 X+ u3 u5 h0+ h2+ M6 M7 S01 J5 Scg Sac S48 S8a z0 Z3 Z1 x0+ H3+ H1+ x1+ x2+ x3+",
+    0: "G2 F0 y d4 C4 up d5 C5 L0 F1 p0 n0 n2 ag F3 p1 A0 n1 L1 R4 R5 I7 I6 A1 p3 mg n3 j0 k0 j1 k1 K2 K3 K4 J0 K5 b7 K6 J1 K7 J2 J3 K9 M7 b6 S01 M6 J5 A2 u0 K8 u1 s14 u2 Scg S48 u3 u4 u5 h0+ h2+ X+ sac H1+ S8a H3+ z0 Z3 Z1 x0+ x1+ x2+ x3+",
+    6: "G2 F0 d4 d5 L0 C4 y C5 F1 p0 l1 F3 n0 p3 n2 P1 R4 R5 A0 A1 A2 n1 n3 j0 L3 A3 k0 j1 k1 K2 K3 K4 J0 K5 K6 J1 K7 J2 J3 K8 u0 o0 S04 o1 u1 s48 O08 u2 scg S8c O8g",
 }
 
 
@@ -91,6 +88,9 @@ def rank_program(g, core, T, topo):
     def tt(out, in0, in1, op):
         emit("v", lambda: g.vector.tensor_tensor(out[0], in0[0], in1[0], op), reg(in0, in1), out[1])
 
+    def scan(out, d0, d1, op0, op1, first=0.0):
+        emit("v", lambda: g.vector.tensor_tensor_scan(out[0], d0[0], d1[0], val(first), op0, op1), reg(d0, d1, first), out[1])
+
     def cp(out, in0):
         emit("v", lambda: g.vector.tensor_copy(out[0], in0[0]), in0[1], out[1])
 
@@ -127,7 +127,7 @@ def rank_program(g, core, T, topo):
     def store(dst, name, c0, c1):
         return [(T[dst][b:b + n, c0:c1], T[name][a:a + n, c0:c1], [(name, c0, c1, None)], []) for a, b, n in rot(16)]
 
-    def torow(name, c0, row, regions):
+    def torow(name, c0, row, regions=(0, 1)):
         return [(T.mw[row:128:16, r * W:(r + 1) * W], T[name][:, c0:c0 + LW], [(name, c0, c0 + LW, None)], [("mw", r * W, (r + 1) * W, row)]) for r in regions]
 
     peers = [T.cores[(rank + d) % N] for d in range(1, N)]
@@ -136,20 +136,31 @@ def rank_program(g, core, T, topo):
         mask &= topo.mask(core, c)
     neng = bin(mask).count("1")
 
-    def exchange(k):
-        name = ("xa", "xb")[k % 2]
+    ns = [0]
+
+    def send(src, dsts):
+        k = ns[0]
+        ns[0] += 1
         ids = [DstId(rid=topo.addr(c)[0], pnc=topo.addr(c)[1]) for c in peers]
-        dsts = [T[name][:, V + d * GH:V + (d + 1) * GH] for d in range(N - 1)]
         emit("g", lambda: g.remote_dma_fused([RemoteDMATransfer(dst_ids=ids, dma_engine_mask=mask, remote_sem=T.sem["ar%d" % k],
-                                                                src=T[name][:, 0:GH], dsts=dsts)], local_sem=T.sem["lo%d" % k]),
-             [(name, 0, GH, None)], [], "r", "lo%d" % k, neng)
-        emit("x", None, [], [(name, V, W, None)], "a", "ar%d" % k, neng * (N - 1))
+                                                                src=src[0], dsts=[d[0] for d in dsts])], local_sem=T.sem["lo%d" % k]),
+             src[1], [], "r", "lo%d" % k, neng)
+        emit("x", None, [], reg(*dsts), "a", "ar%d" % k, neng * (N - 1))
+
+    def gblock(k, d, n=1):
+        return ap("gw", CH * k + GH * d, CH * k + GH * (d + n))
+
+    def goffs(t, d):
+        return ap("gx", 16 * (3 * (t % 2) + d), 16 * (3 * (t % 2) + d + 1))
 
     def col(k):
         return ap("col", k, k + 1)
 
-    def bmat(k, j, p=128):
-        return ap("bs", 144 * k + 15 - j, 144 * k + 143 - j, p=p)
+    def oh(k):
+        return ap("oh", k, k + 1)
+
+    def bmat(k, j):
+        return ap("bs", 144 * k + 15 - j, 144 * k + 143 - j)
 
     def ident(k):
         return ap("ids", 128 * k, 128 * k + 128)
@@ -157,14 +168,20 @@ def rank_program(g, core, T, topo):
     def mat(k, p=128):
         return ap("ms", 128 * k, 128 * k + 128, p=p)
 
-    B1, BH, BF, BO2, BO3, B8 = range(6)
-    I1, INEG, I4096, IBIG, I304, I16TH, I4864, I16, IHUGE = range(9)
-    ONES, TRI, A1, ALL, E8, MGE, MLE, MTMP = range(8)
-    P, PM, C0, C15, G0, G15, WF, WA, WB, WO2, WC, WO3, JJ, NB = range(14)
+    def lst(name, k=0, c0=0, c1=256):
+        return ap(name, LW * k + c0, LW * k + c1)
 
-    def jf(k, c0=0, c1=273, step=1):
-        return ap("jf", 288 * k + c0, 288 * k + c1, step, p=8)
-    LM, NE, N2, THR, TNEG, TPOS, NLM = range(7)
+    def mcol(k):
+        return 3 * CH * (k // 2) + 512 * (k % 2)
+
+    B1, BH, BU, BU6, BC5, BC6 = range(6)
+    I1, INEG, ICH, I304, I16TH, I4864, INU, INH, I16, IHUGE = range(10)
+    BLK, SCO, ALL, E8, MGE, MTMP = range(6)
+    P, PM, C0, C15, G0, WA, WB, WC, WD, WE, JJ, NB, N3, VB, SC = range(15)
+    LIM, TH, TMP = 0, 256, 512
+    NE, THR, LM = 0, 17, 34
+    D2, E2, W3, RQ, M13 = range(0, 80, 16)
+    C5, BASE = 6, 7
 
     dmas("y", load("xa", 0, "x0", 0, GH))
     dmas("s", load("sgi", 0, "sg", 0, 273, 1) + load("lmi", 0, "lm", 0, 273, 1))
@@ -173,100 +190,128 @@ def rank_program(g, core, T, topo):
     dmas("y", load("xa", V // 2, "x0", V // 2, V))
     iota(ap("ic"), [[1, 144]], 0, 0)
     iota(ap("pi", 0, 1), [[1, 1]], 0, 1)
-    iota(ap("col", G0, G15 + 1), [[15, 2]], 0, 16)
+    iota(col(G0), [[1, 1]], 0, 16)
     iota(mat(MGE), [[16, 8], [0, 16]], 0, 0)
     iota(ap("pt", 256, LW), [[16, 48]], 2048, 0)
-    exchange(0)
-    iota(ap("c16"), [[0, 16], [1, 16]], 0, 0)
-    iota(ap("k16"), [[16, 256]], 0, 0)
-    iota(ap("mw", W, 2 * W), [[0, W]], 0, 0)
-    fill(ap("mw", 0, W // 2), 0.0)
+    send(ap("xa", 0, GH), [ap("xa", V + d * GH, V + (d + 1) * GH) for d in range(N - 1)])
+    iota(ap("k16"), [[0, 4], [16, 64]], 0, 0)
+    iota(ap("mw", 2 * V, 2 * W), [[0, 2 * (W - V)]], 0, 0)
     cp(col(P), ap("pi", 0, 1))
     ts(ap("pi", 1, 2), ap("pi", 0, 1), 15, A.bitwise_and)
-    cp(ap("icf"), ap("ic", 0, 16))
     ts(ident(I1), ap("ic", 0, 128), col(P), A.is_equal)
+    fill(col(WE), 1.0 / 64)
     cp(col(PM), ap("pi", 1, 2))
-    act(ap("mw", W // 2, W), ap("mw", 0, W // 2), F.Copy)
-    for k, w in ((INEG, -1.0), (I304, float(LW)), (I16TH, 0.0625), (I4096, float(V)), (I4864, float(W)), (I16, 16.0), (IHUGE, -131072.0)):
+    cp(ap("icf"), ap("ic", 0, 16))
+    for k, w in ((INEG, -1.0), (ICH, float(CH)), (I304, float(LW)), (I16TH, 0.0625)):
         act(ident(k), ident(I1), F.Copy, scale=w)
-    for k in range(8):
-        act(ap("bt", LW * k + 256, LW * k + LW), ap("mw", 0, 48), F.Copy)
-    act(mat(ALL), ap("mw", 0, 128), F.Identity, bias=1.0)
-    act(ap("bt", 7 * LW, 7 * LW + 256), ap("mw", 0, 256), F.Identity, bias=1.0)
-    act(ap("xo", 0, V // 2), ap("xa", 0, V // 2), F.Copy)
+    act(mat(ALL), ident(I16TH), F.Identity, bias=col(WE), scale=0.0)
     fill(col(NB), -16.5)
     tt(col(C0), col(P), col(PM), A.subtract)
-    ts(ap("oh"), ap("icf"), col(PM), A.is_equal)
-    cp(ap("ofc"), ap("icf"))
-    ts(col(JJ), col(PM), -7.5, A.add)
+    fill(ap("seg"), 1.0)
     ts(col(C15), col(C0), 15.0, A.add)
-
-    def oh(k):
-        return ap("oh", k, k + 1)
-    ts(col(WF), oh(3), oh(4), A.add, -2 * BIG, A.mult)
-    ts(col(WA), oh(2), -BIG, A.mult, oh(0), A.add)
-    ts(col(WB), oh(6), 0.0625, A.mult, oh(1), A.add)
-    ts(col(WC), oh(2), oh(5), A.add)
-    emit("v", lambda: g.vector.tensor_reduce(col(WO3)[0], T.oh[:, 7:11], AxisListType.X, A.add), [("oh", 7, 11, None)], col(WO3)[1])
-    cp(ap("of1"), ap("adi"))
-    ts(ap("s0"), ap("adi"), -S0, A.add)
+    cp(ap("ofc"), ap("icf"))
+    fill(ap("seg", 0, 256, 16), 0.0)
     ts(ap("bs", 0, 144), ap("ic"), col(C15), A.is_equal)
     ts(ap("bs", 144 * BH, 144 * BH + 144), ap("ic"), col(C15), A.is_equal, 0.5, A.mult)
-    ts(ap("bs", 144 * B8, 144 * B8 + 144), ap("ic"), col(G15), A.is_equal)
-    ts(mat(E8), mat(MGE), col(G0), A.is_equal)
-    ts(mat(ONES), mat(MGE), col(C0), A.is_equal, -1.0, A.mult)
-    ts(mat(MTMP), mat(MGE), col(C0), A.is_equal, -1.0 / 32, A.mult)
-    ts(col(WO2), col(WA), col(WB), A.add, col(WF), A.add)
-    tt(col(WO3), col(WO3), col(WC), A.add)
-    ts(ap("pt", 0, 256), ap("s0"), MAGIC, A.add, MAGIC, A.subtract)
-    ts(jf(LM), ap("lmi", 0, 273, p=8), 0.0, A.add)
-    ts(jf(NE), ap("sgi", 0, 273, p=8), 1.0, A.not_equal, 99.0, A.mult)
-    ts(jf(N2), ap("sgi", 0, 273, p=8), 2.0, A.not_equal)
-    tt(ap("pj", 0, 256), ap("s0"), ap("pt", 0, 256), A.subtract)
-    tt(jf(THR), jf(LM), jf(N2), A.mult)
-    act(jf(NLM, 256, 272), jf(LM, 256, 272), F.Copy, scale=-1.0)
-    ts(col(WA), col(PM), float(GH), A.add)
-    act(ap("v0", 0, 16), ap("icf"), F.Identity, bias=col(WA), scale=16.0)
-    ts(mat(MLE), ap("ic", 0, 128), col(P), A.is_ge)
-    ts(jf(TNEG, 256, 272), jf(THR, 256, 272), -1.0 / 32, A.mult, -1.0 / 64, A.add)
-    ts(jf(TPOS, 0, 256), jf(THR, 0, 256), 1.0 / 32, A.mult, 1.0 / 64, A.add)
-    tt(mat(TRI), mat(ONES), mat(MLE), A.mult)
-    dmas("y", [(o, i, [("xa", GH, V, None)], wr) for o, i, rd, wr in load("w2", 0, "xi", 0, GH) + load("w2", GH + V, "xi", 0, V)])
-    mm(ap("p0", 0, 256), mat(E8, 8), jf(NE, 0, 256), True, True)
-    for i in range(16):
-        mm(ap("p1", 0, 16), bmat(B8, i, 8), jf(LM, i, 256, 16), i == 0, i == 15)
-    mm(ap("p1", 16, 32), mat(E8, 8), jf(NE, 256, 272), True, True)
-    mm(ap("p1", 32, 48), mat(E8, 8), jf(TNEG, 256, 272), True, True)
-    mm(ap("p1", 48, 64), mat(E8, 8), jf(NLM, 256, 272), True, True)
-    mm(ap("p1", 64, 65), mat(E8, 8), jf(THR, 272, 273), True, True)
-    mm(ap("p1", 65, 66), mat(E8, 8), jf(LM, 272, 273), True, True)
-    mm(ap("p1", 66, 67), mat(E8, 8), jf(NE, 272, 273), True, True)
-    mm(ap("p3", 0, 256), ident(I304), ap("pj", 0, 256), True, False)
-    mm(ap("p3", 0, 256), ident(I16TH), ap("pt", 0, 256), False, True)
-    ts(ap("dia"), ap("c16"), col(PM), A.is_equal)
-    for k, w in ((BO2, WO2), (BO3, WO3)):
-        ts(ap("bs", 144 * k, 144 * k + 144), ap("ic"), col(C15), A.is_equal, col(w), A.mult)
-    tt(mat(A1), mat(MTMP), ident(INEG), A.add)
-    for k in range(3):
-        act(ap("pj", LW * k + 256, LW * k + LW), ap("ic", 0, 48), F.Identity, bias=col(JJ), scale=0.0)
+    ts(col(JJ), col(PM), -7.5, A.add)
+    act(lst("pj", 0, 256, LW), ap("ic", 0, 48), F.Identity, bias=col(JJ), scale=0.0)
+    act(lst("bt", 0, 256, LW), ap("ic", 0, 48), F.Copy, scale=0.0)
     for k in (1, 2):
-        act(ap("pt", LW * k + 256, LW * k + LW), ap("pt", 256, LW), F.Copy)
-    act(ap("th", 0, 67), ap("p1", 0, 67), F.Copy)
-    act(ap("t9"), ap("p0", 0, 256), F.Copy)
-    ts(ap("of2"), ap("p3", 0, 256), 2408.0, A.add)
-    tt(ap("th", 16, 32), ap("th", 16, 32), ap("th", 0, 16), A.add)
-    ts(ap("m13"), ap("icf"), 0.0, A.mult, ap("th", 66, 67), A.is_equal)
-    dmas("y", torow("pj", 0, 0, (0, 1)) + torow("pt", 0, 1, (0, 1)) + torow("bt", 7 * LW, 5, (0, 1)))
+        act(lst("pj", k, 256, LW), lst("pj", 0, 256, LW), F.Copy)
+        act(lst("pt", k, 256, LW), lst("pt", 0, 256, LW), F.Copy)
+    for k in (1, 2, 3, 4, BASE):
+        act(lst("bt", k, 256, LW), lst("bt", 0, 256, LW), F.Copy)
+    for k, w in ((I4864, float(W)), (INH, -BIG / 2), (INU, -U), (I16, 16.0), (IHUGE, -131072.0)):
+        act(ident(k), ident(I1), F.Copy, scale=w)
+    act(ap("i32"), ident(I1), F.Copy, scale=BIG)
+    ts(mat(MTMP), ap("ic", 0, 128), col(P), A.is_ge, 32.0, A.mult)
+    ts(mat(E8), mat(MGE), col(G0), A.is_equal)
+    ts(ap("js", NE, NE + 17, p=8), ap("sgi", 256, 273, p=8), 1.0, A.not_equal)
+    tt(mat(MTMP), mat(MTMP), ident(ICH), A.add)
+    ts(ap("js", THR, THR + 17, p=8), ap("sgi", 256, 273, p=8), 2.0, A.not_equal)
+    ts(ap("js", LM, LM + 17, p=8), ap("lmi", 256, 273, p=8), 0.0, A.add)
+    ts(mat(MTMP), mat(MTMP), 1.0, A.add, -U, A.mult)
+    ts(mat(BLK), mat(MGE), col(C0), A.is_equal)
+    tt(ap("js", THR, THR + 17, p=8), ap("js", THR, THR + 17, p=8), ap("js", LM, LM + 17, p=8), A.mult)
+    ts(ap("jf", TMP, TMP + 256, p=8), ap("sgi", 0, 256, p=8), -500.0, A.mult, -519.5, A.max)
+    tt(mat(SCO), mat(MTMP), mat(BLK), A.mult)
+    mm(ap("p1", 0, 51), mat(E8, 8), ap("js", 0, 51, p=8), True, True)
+    ts(ap("jf", LIM, LIM + 256, p=8), ap("lmi", 0, 256, p=8), -1.0, A.mult, -0.5, A.add)
+    ts(ap("jf", TH, TH + 256, p=8), ap("jf", TMP, TMP + 256, p=8), 520.0, A.add, U, A.mult)
+    cp(ap("of1"), ap("adi"))
+    act(ap("th", 0, 51), ap("p1", 0, 51), F.Copy, scale=0.0625)
+    ts(ap("s0"), ap("adi"), -S0, A.add)
+    ts(ap("oh"), ap("icf"), col(PM), A.is_equal)
+    ts(ap("dec"), ind(ap("th", 0, 16), ap("ofc")), -1.0, A.mult)
+    ts(ap("up", M13, M13 + 16), ap("icf"), 0.0, A.mult, ap("th", NE + 16, NE + 17), A.is_equal)
+    fill(ap("dec", 0, 256, 16), -99.0)
+    first = ORDER[1].split()
+    for c in range(4):
+        if "F%d" % c in first:
+            act(ap("xo", CH * c, CH * c + CH), ap("xa", CH * c, CH * c + CH), F.Copy)
+    def initial(c):
+        dmas("y", [(o, i, [("xa", GH, V, None)], wr) for o, i, rd, wr in load("w2", mcol(2 * c) + CH, "xi", CH * c, CH * c + CH)])
+    for c in range(4):
+        initial(c)
+    if "mg" in first:
+        dmas("y", [(o, i, [("xa", GH, V, None)], wr) for k in (1, 2) for o, i, rd, wr in load("gw", k * GH, "xi", 0, GH)])
+        ts(ap("v0", 0, 16), ap("icf"), 16.0, A.mult, col(PM), A.add)
+        act(ap("kq"), ap("v0", 0, 16), F.Copy, scale=4.0)
+        fill(ap("w2", 0, GH), 0.0)
+    if "D" in first:
+        for k in (0, 1, 3, 4):
+            iota(gblock(k, 3), [[0, GH]], 0, 0)
+        send(ap("w2", CH, CH + GH), [gblock(4, d) for d in range(N - 1)])
 
-    for t in range(1, STEPS + 1):
+    def spread():
+        dmas("y", [(gblock(k, 0, 3)[0], gblock(4, 0, 3)[0], gblock(4, 0, 3)[1], gblock(k, 0, 3)[1]) for k in (5, 1, 2)])
+
+    ts(lst("pt"), ap("s0"), MAGIC, A.add, MAGIC, A.subtract)
+    ts(col(WB), oh(3), oh(4), A.add, -2.0, A.mult)
+    ts(col(WE), oh(0), oh(1), A.add, U, A.mult)
+    tt(lst("pj"), ap("s0"), lst("pt"), A.subtract)
+    ts(col(WC), col(WB), oh(2), A.subtract, col(WE), A.add)
+    fill(col(VB), -64.0)
+    fill(ap("jf", TMP, TMP + 256, p=8), 0.5)
+    mm(ap("p5", 0, 256), ident(I304), lst("pj"), True, False)
+    mm(ap("p5", 0, 256), ident(I16TH), lst("pt"), False, True)
+    ts(ap("bs", 144 * BU, 144 * BU + 144), ap("ic"), col(C15), A.is_equal, col(WC), A.mult)
+    ts(ap("of2"), ap("p5", 0, 256), 2408.0, A.add)
+    act(lst("bt", C5, 0, LW), ap("xa", 0, LW), F.Copy, scale=0.0)
+
+    def later():
+        ts(col(WB), oh(6), U / 16, A.mult, col(WC), A.add)
+        ts(col(WD), oh(2), oh(5), A.add)
+        ts(col(WE), oh(7), col(WD), A.add)
+        for k, w in ((BU6, WB), (BC5, WD), (BC6, WE)):
+            ts(ap("bs", 144 * k, 144 * k + 144), ap("ic"), col(C15), A.is_equal, col(w), A.mult)
+
+    def step(t):
         cur, nxt = ("xa", "xb")[(t - 1) % 2], ("xa", "xb")[t % 2]
-        names, last = t > 1, t == STEPS
-        order = ORDER[1 if t == 1 else 0].split()
-        cmps = [c for c in range(4) if "C%d" % (2 * c) in order or "P%d" % c in order]
+        names, raw, last = t > 1, t > 2, t == STEPS
+        order = ORDER.get(t, ORDER[0]).split()
+        signs = [c for c in range(4) if "C%d" % (2 * c) in order or "P%d" % c in order]
         slot = 1 + (t % 2)
-        b = ap("bt", LW * (t - 1), LW * (t - 1) + 256)
+        b = lst("bt", t - 1)
 
-        free, held = list(BANKS), {}
+        def wide(name, c0, c1, st=1):
+            if t == 1 and name in ("cm", "dd"):
+                o = V if name == "dd" else 0
+                return ap("mw", o + c0, o + c1, st)
+            return ap(name, c0, c1, st)
+
+        def again(q, c):
+            gather(q, ap("w2", mcol(2 * c) + 2 * CH, mcol(2 * c) + 3 * CH), ap("w2", mcol(2 * c) + CH, mcol(2 * c) + 2 * CH))
+
+        def againdma(c):
+            o, i = ap("w2", mcol(2 * c) + 2 * CH, mcol(2 * c) + 3 * CH), ap("w2", mcol(2 * c) + CH, mcol(2 * c) + 2 * CH)
+            dmas("y", [(o[0], i[0], i[1], o[1])])
+
+        def chunk(name, c):
+            return wide(name, CH * c, CH * c + CH)
+
+        def half(name, k):
+            return wide(name, 512 * k, 512 * k + 512)
 
         def gather(q, o, i):
             if q == "v":
@@ -275,235 +320,285 @@ def rank_program(g, core, T, topo):
                 act(o, i, F.Copy)
 
         def g1(q, c):
-            gather(q, ap("dd", 1024 * c, 1024 * c + 1024), ind(ap(cur), ap("of1", 64 * c, 64 * c + 64)))
+            gather(q, chunk("dd", c), ind(ap(cur), ap("of1", 64 * c, 64 * c + 64)))
 
         def g2(q, c):
-            gather(q, ap("go", 1024 * c, 1024 * c + 1024), ind(ap("mw"), ap("of2", 64 * c, 64 * c + 64)))
+            gather(q, chunk("go", c), ind(ap("mw"), ap("of2", 64 * c, 64 * c + 64)))
 
-        def own(q, c):
-            o, i = ap("xo", 1024 * c, 1024 * c + 1024), ap(cur, 1024 * c, 1024 * c + 1024)
-            if t == 1 and c < 2:
-                return
-            if c in OWN_DMA and names:
-                dmas("y", [(o[0], i[0], i[1], o[1])])
-            else:
-                gather(q, o, i)
+        def own(c):
+            o, i = chunk("xo", c), chunk(nxt, c)
+            dmas("y", [(o[0], i[0], i[1], o[1])])
 
         def fused(c):
-            tt(ap("dd", 1024 * c, 1024 * c + 1024), ind(ap(cur), ap("of1", 64 * c, 64 * c + 64)), ap("xo", 1024 * c, 1024 * c + 1024), A.subtract)
+            tt(chunk("dd", c), ind(ap(cur), ap("of1", 64 * c, 64 * c + 64)), chunk("xo", c), A.subtract)
 
-        def cmpf(q, c):
-            o, i = ap("cm", 1024 * c, 1024 * c + 1024), ap("dd", 1024 * c, 1024 * c + 1024)
+        def compare(q, o, i):
             if q == "s":
                 act(o, i, F.Sign, bias=col(NB), scale=-1.0)
             else:
                 ts(o, i, -16.5, A.is_lt, 0.5, A.subtract)
 
-        def relu(q, k):
-            o = ap("w2", GH + 512 * k, GH + 512 * k + 512) if "A%d" % (k // 2) in order else ap("rr", 512 * k, 512 * k + 512)
-            i = ap("dd", 512 * k, 512 * k + 512)
+        def cmpf(q, c):
+            compare(q, chunk("cm", c), chunk("dd", c))
+
+        def relu(q, c):
+            c0 = GH if c == 0 and "mg" in order else 0
+            o, i = ap("w2", mcol(2 * c) + c0, mcol(2 * c) + CH), wide("dd", CH * c + c0, CH * c + CH)
             if q == "s":
                 act(o, i, F.Relu)
             else:
                 ts(o, i, 0.0, A.max)
 
+        def ghosty():
+            mm(ap("p5", 0, GH), ident(I1), ap(cur, 0, GH), True, False)
+            mm(ap("p5", 0, GH), ident(I1), wide("dd", 0, GH), False, True)
+
+        def ghostmax():
+            tt(ap("gw", 0, GH), ap("p5", 0, GH), ap(cur, 0, GH), A.max)
+
+        def relu2(q, k):
+            if q == "s":
+                act(half("rr", k), half("dd", k), F.Relu)
+            else:
+                ts(half("rr", k), half("dd", k), 0.0, A.max)
+
+        def twin(q, c):
+            gather(q, chunk("xo", c), chunk(nxt, c))
+
+        def gtwin(c):
+            o, i = chunk("xo", c), chunk(nxt, c)
+            emit("g", lambda: g.affine_select(o[0], i[0], [[0, CH]], A.is_gt, 0.0, 1, 0), i[1], o[1])
+
         def adddma(c):
-            o, i = ap("w2", GH + 1024 * c, GH + 1024 * c + 1024), ap(cur, 1024 * c, 1024 * c + 1024)
+            c0 = GH if c == 0 and "mg" in order else 0
+            o, i = ap("w2", mcol(2 * c) + c0, mcol(2 * c) + CH), ap(cur, CH * c + c0, CH * c + CH)
             sem = "dm%d" % nd[0]
             nd[0] += 1
             emit("g", lambda: g.dma_start(o[0], i[0], accum_op=A.add), i[1] + o[1], o[1], "d", sem, 16)
 
+        def bank(kind, k):
+            return ap("p%d" % (6 + k % 2))
+
         def ypsum(k):
-            held["y", k] = free.pop(0)
-            mm(ap("p%d" % held["y", k]), ident(I1), ap("dd", 512 * k, 512 * k + 512), True, "e%d" % k not in order)
+            if "F%d" % (k // 2) in order:
+                mm(bank("y", k), ident(I1), half(cur, k), True, False)
+                mm(bank("y", k), ident(I1), half("dd", k), False, True)
+            else:
+                mm(bank("y", k), ident(I1), half("dd", k), True, True)
 
         def mx(k):
-            tt(ap("w2", GH + 512 * k, GH + 512 * k + 512), ap("p%d" % held["y", k]), ap(cur, 512 * k, 512 * k + 512), A.max)
-            if "e%d" % k not in order:
-                free.append(held["y", k])
+            tt(ap("w2", mcol(k), mcol(k) + 512), bank("y", k), half(cur, k), A.max)
 
         def dpsum(k):
-            held["d", k] = free.pop(0)
-            mm(ap("p%d" % held["d", k]), ident(INEG), ap(cur, 512 * k, 512 * k + 512), True, False)
-            mm(ap("p%d" % held["d", k]), ident(I1), ap("dd", 512 * k, 512 * k + 512), False, True)
-
-        def dafter(k):
-            held["d", k] = held["y", k]
-            mm(ap("p%d" % held["d", k]), ident(INEG), ap(cur, 512 * k, 512 * k + 512), False, True)
+            mm(bank("d", k), ident(INEG), half(cur, k), True, False)
+            mm(bank("d", k), ident(I1), half("dd", k), False, True)
 
         def cmp_(q, k):
-            o, i = ap("cm", 512 * k, 512 * k + 512), ap("p%d" % held["d", k])
-            if q == "s":
-                act(o, i, F.Sign, bias=col(NB), scale=-1.0)
-            else:
-                ts(o, i, -16.5, A.is_lt, 0.5, A.subtract)
-            if "R%d" % k not in order or "D%d" % k in order:
-                free.append(held["d", k])
+            compare(q, half("cm", k), bank("d", k))
 
         def rise(k):
-            o = ap("w2", GH + 512 * k, GH + 512 * k + 512) if "A%d" % (k // 2) in order else ap("rr", 512 * k, 512 * k + 512)
-            act(o, ap("p%d" % held["d", k]), F.Relu)
-            free.append(held["d", k])
+            o = ap("w2", mcol(k), mcol(k) + 512) if "A%d" % (k // 2) in order else half("rr", k)
+            act(o, bank("d", k), F.Relu)
 
         def addx(k):
-            held["y", k] = free.pop(0)
-            mm(ap("p%d" % held["y", k]), ident(I1), ap(cur, 512 * k, 512 * k + 512), True, False)
-            mm(ap("p%d" % held["y", k]), ident(I1), ap("rr", 512 * k, 512 * k + 512), False, True)
+            mm(bank("y", k), ident(I1), half(cur, k), True, False)
+            mm(bank("y", k), ident(I1), half("rr", k), False, True)
 
         def mxs(k):
-            act(ap("w2", GH + 512 * k, GH + 512 * k + 512), ap("p%d" % held["y", k]), F.Copy)
-            free.append(held["y", k])
+            act(ap("w2", mcol(k), mcol(k) + 512), bank("y", k), F.Copy)
 
         def pick(out, k, src, c, start, stop):
             for j in range(16):
-                mm(out, bmat(k, j), ap(src, 1024 * c + j, 1024 * c + 1024, 16), start and j == 0, stop and j == 15)
+                mm(out, bmat(k, j), wide(src, CH * c + j, CH * c + CH, 16), start and j == 0, stop and j == 15)
 
-        def void(c):
-            ts(ap("rw", 64 * c, 64 * c + 64), ap("p3", 64 * c, 64 * c + 64), -1.5 * BIG, A.is_lt, 9.0, A.mult)
+        def opennames():
+            mm(ap("p3", 0, 256), ident(INU), lst("pt"), True, False)
+            mm(ap("p3", 0, 256), ident(INU), lst("pj"), False, False)
+            mm(ap("p3", 0, 256), mat(E8, 8), ap("jf", TMP, TMP + 256, p=8), False, False)
+            if t == 5:
+                mm(ap("p4", 0, 256), ident(I1), lst("bt", C5), True, False)
+            if last:
+                mm(ap("p4", 0, 256), ident(I16), lst("pt", 3 - slot), True, False)
+                mm(ap("p4", 0, 256), ident(I16), lst("pj", 3 - slot), False, False)
 
-        def count(c):
-            o = ap("p%d" % (c % 2), 0, 64)
-            pick(o, BH if c in cmps else B1, "cm", c, True, not names)
-            if names:
-                mm(o, ident(I1), ap("rw", 64 * c, 64 * c + 64), False, True)
+        picked = []
 
         def nexts(c):
-            if names:
-                o = ap("p3", 64 * c, 64 * c + 64)
-                mm(o, ident(INEG), ap("pt", 64 * c, 64 * c + 64), True, False)
-                mm(o, ident(INEG), ap("pj", 64 * c, 64 * c + 64), False, False)
-                pick(o, BO2, "go", c, False, True)
-            if t == 5:
-                pick(ap("p4", 64 * c, 64 * c + 64), BO3, "go", c, True, True)
-            if t == 6:
-                pick(ap("p4", 64 * c, 64 * c + 64), BO3, "go", c, False, False)
+            picked.append(c)
+            pick(ap("p3", 64 * c, 64 * c + 64), BU6 if last else BU, "go", c, False, len(picked) == 4)
+            if t >= 5:
+                pick(ap("p4", 64 * c, 64 * c + 64), BC6 if last else BC5, "go", c, False, t == 5 and len(picked) == 4)
 
-        def crash(c):
-            o = ap("p%d" % (c % 2), 0, 64)
-            ts(ap("cr", 64 * c, 64 * c + 64), o, 0.5, A.is_gt)
-            tt(ap("cr1", 64 * c, 64 * c + 64), o, ap("t9", 64 * c, 64 * c + 64), A.is_gt)
+        def void():
+            act(ap("rw"), ap("p3", 0, 256), F.Relu, bias=col(VB), scale=-64.0)
 
-        def sel(q, c0, c1):
-            gather(q, ap(nxt, c0, c1), ind(ap("w2", GH), ap("idx", c0 // 16, c1 // 16)))
+        def count(c):
+            o = ap("p0", 64 * c, 64 * c + 64) if c < 3 else ap("p1", 0, 64)
+            pick(o, BH if c in signs else B1, "cm", c, True, not raw)
+            if raw:
+                mm(o, ident(I1), ap("rw", 64 * c, 64 * c + 64), False, True)
+
+        def part(h, k):
+            c0, c1 = ((0, 192), (192, 256), (0, 256))[h]
+            n = c1 - c0
+            cnt, n1, score, at = ((ap("p0", 0, n), ap("p0", 256, 256 + n), ap("p2", 0, n), ap("p0", 0, n)) if h != 1 else
+                                  (ap("p1", 0, n), ap("p1", 64, 64 + n), ap("p1", 128, 128 + n), ap("p1", 192, 192 + n)))
+            if h == 1 and "K7" in order:
+                score = ap("p2", c0, c1)
+            tot, head = ap("n2", c0 + 15, c1, 16), ap("d1", c0, c1, 16)
+
+            def u(c, name="up"):
+                return ap(name, c + c0 // 16, c + c1 // 16)
+            if k == 0:
+                ts(ap("cr", c0, c1), cnt, 0.5, A.is_gt)
+                mm(n1, mat(E8, 8), ap("jf", LIM + c0, LIM + c1, p=8), True, False)
+                mm(n1, mat(BLK), ap("cr", c0, c1), False, True)
+                mm(score, mat(E8, 8), ap("jf", TH + c0, TH + c1, p=8), True, False)
+                mm(score, mat(SCO), ap("cr", c0, c1), False, True)
+            elif k == 1:
+                ts(ap("d1", c0, c1), n1, 0.0, A.is_gt, 0.0625, A.mult)
+            elif k == 2:
+                scan(ap("n2", c0, c1), ap("seg", c0, c1), ap("d1", c0, c1), A.mult, A.add)
+            elif k == 3:
+                tt(u(D2), tot, u(LM, "th"), A.is_gt)
+                tt(u(E2), tot, u(THR, "th"), A.is_gt)
+            elif k == 4:
+                scan(u(W3), u(M13), u(D2), A.mult, A.add, ap("up", W3 + 11, W3 + 12) if h == 1 else 0.0)
+                tt(u(RQ), u(E2), head, A.max)
+            elif k == 5:
+                tt(head, u(W3), u(RQ), A.max)
+            elif k == 6:
+                scan(ap("zs", c0, c1), ap("dec", c0, c1), ap("d1", c0, c1), A.add, A.max)
+            elif k == 7:
+                tt(ap("bp", c0, c1), score, ap("zs", c0, c1), A.is_lt)
+                if h != 1 and "mg" in order:
+                    mm(ap("p0", 448, 464), ident(I1), ap("kq"), True, False)
+                    mm(ap("p0", 448, 464), ident(ICH), ap("bp", 0, 16), False, True)
+                mm(at, ident(I1), ap("k16", c0, c1), True, False)
+                mm(at, ident(ICH), ap("bp", c0, c1), False, True)
+            elif k == 8:
+                e = 16 if h != 1 and ("j9" in order or "K9" in order) else 0
+                ts(ap("idx", c0 + e, c1), ap(at[1][0][0], e + 192 * (h == 1), n + 192 * (h == 1)), col(PM), A.add, col(SC), A.add)
+            else:
+                ts(ap("ix0"), ap("p0", 448, 464), col(SC), A.add, 0.25, A.mult)
+
+        def judges(k):
+            def u(c):
+                return ap("up", c, c + 16)
+            whole_ = ap("p1" if "K7" in order else "p2", 256, 257)
+            if k == 0:
+                emit("v", lambda: g.vector.tensor_reduce(col(N3)[0], u(D2)[0], AxisListType.X, A.add), u(D2)[1], col(N3)[1])
+            elif k == 1:
+                ts(ap("ed", 0, 2), ap("th", THR + 16, LM + 17, 17), 16.0, A.mult, col(N3), A.is_lt)
+                mm(whole_, mat(ALL), ap("ed", 1, 2), True, False)
+                mm(whole_, ident(I1), ap("ed", 0, 1), False, True)
+            elif k == 2:
+                ts(col(SC), whole_, 0.875, A.is_gt, float(CH), A.mult)
+            elif k == 3:
+                ts(b, ap("bp"), col(SC), A.add, 0.5, A.is_gt)
+                if not last:
+                    dmas("y", torow("bt", LW * (t - 1), 2, (0,)) + torow("bt", LW * (t - 1), 3 + t % 2, (1,)))
+            elif k == 4:
+                send(ap("idx", 0, 16), [goffs(t, d) for d in range(N - 1)])
+            else:
+                send(ap(nxt, 0, GH), [ap(nxt, V + d * GH, V + (d + 1) * GH) for d in range(N - 1)])
+
+        def maxima():
+            send(ap("w2", 0, GH), [gblock(3 * (t % 2), d) for d in range(N - 1)])
+
+        def ghosts(q, d):
+            c0 = 3 * CH * (t % 2) + GH * d
+            gather(q, ap(nxt, V + GH * d, V + GH * d + GH), ind(ap("gw", c0, c0 + 2 * CH + GH), goffs(t, d)))
+
+        def sel(q, w):
+            c0, c1 = 256 * int(w[0], 17), 256 * int(w[1], 17)
+            m = mcol(2 * (c0 // CH))
+            if c1 == GH and "mg" in order:
+                gather(q, ap(nxt, 0, GH), ind(ap("gw", 0, 3 * GH), ap("ix0")))
+                return
+            gather(q, ap(nxt, c0, c1), ind(ap("w2", m, m + 3 * CH), ap("idx", c0 // 16, c1 // 16)))
 
         def update():
-            items = []
-            if 3 <= t <= 5:
-                items += torow("pj", LW * (3 - slot), 0, (0, 1)) + torow("pt", LW * (3 - slot), 1, (0, 1))
-            if t <= 5:
-                items += torow("bt", LW * (t - 2), 5 + t, (0, 1))
-                dmas("y", items)
-
-        if last:
-            mm(ap("p4", 0, 256), ident(I16), ap("pt", LW * (3 - slot), LW * (3 - slot) + 256), True, False)
-            mm(ap("p4", 0, 256), ident(I16), ap("pj", LW * (3 - slot), LW * (3 - slot) + 256), False, False)
-
-        def j1():
-            for i in range(16):
-                mm(ap("p1", 0, 16), bmat(B1, i), ap("cr", i, 256, 16), i == 0, i == 15)
-
-        def q0():
-            mm(ap("p2", 0, 256), mat(E8, 8), jf(TPOS, 0, 256), True, False)
-
-        def q1():
-            mm(ap("p2", 0, 256), mat(A1), ap("cr"), False, False)
-            mm(ap("p2", 0, 256), mat(TRI), ap("cr1"), False, False)
-            mm(ap("p0", 0, 256), ident(I1), ap("k16"), True, False)
-
-        def j2():
-            tt(ap("d1", 0, 16), ap("p1", 0, 16), ap("th", 0, 16), A.is_gt)
-            tt(ap("d1", 16, 32), ap("p1", 0, 16), ap("th", 16, 32), A.is_gt)
-            mm(ap("p1", 32, 48), mat(A1), ap("d1", 0, 16), True, False)
-            mm(ap("p1", 32, 48), mat(TRI), ap("d1", 16, 32), False, True)
-            mm(ap("p1", 48, 64), mat(ONES), ap("d1", 0, 16), True, True)
-
-        def j3():
-            tt(ap("bd"), ap("p1", 32, 64), ap("th", 32, 64), A.is_lt)
-            emit("v", lambda: g.vector.tensor_reduce(T.n3[:, 0:1], T.bd[:, 16:32], AxisListType.X, A.add), ap("bd", 16, 32)[1], ap("n3")[1])
-            emit("v", lambda: g.vector.tensor_tensor_scan(T.w3[:, 0:16], T.m13[:, 0:16], T.bd[:, 16:32], 0.0, A.mult, A.add),
-                 reg(ap("m13"), ap("bd", 16, 32)), ap("w3")[1])
-            ts(ap("ed", 0, 2), ap("th", 64, 66), ap("n3", 0, 1), A.is_lt)
-            tt(ap("rs"), ap("bd", 0, 16), ap("w3"), A.add)
-            mm(ap("p1", 64, 65), mat(ALL), ap("ed", 1, 2), True, True)
-            tt(ap("rex"), ind(ap("rs"), ap("ofc")), ap("dia"), A.mult)
-            mm(ap("p2", 0, 256), mat(ONES), ap("rex"), False, True)
-
-        def j4():
-            ts(ap("sc", 0, 1), ap("p1", 64, 65), 63.5, A.is_gt, ap("ed", 0, 1), A.add)
-            if not last:
-                ts(ap("v0", 16, 32), ap("p2", 0, 16), ap("sc", 0, 1), A.is_lt, -float(GH), A.mult)
-                tt(ap("v0", 32, 48), ap("v0", 16, 32), ap("v0", 0, 16), A.add)
-                cp(ap("ix0"), ap("v0", 32, 48))
-                act(ap(nxt, 0, GH), ind(ap("w2", 0, 2 * GH), ap("ix0")), F.Copy)
-                exchange(t)
-
-        def c5():
+            if t == 1:
+                dmas("y", torow("pj", 0, 0, (0,)) + torow("pt", 0, 1, (0,)) + torow("bt", LW * C5, 3, (0,)) + torow("bt", LW * C5, 4, (0,)))
+                return
+            if t == 2:
+                dmas("y", torow("pj", 0, 0, (1,)) + torow("pt", 0, 1, (1,)) + torow("bt", LW * C5, 2, (1,)))
+                return
+            items = torow("pj", LW * (3 - slot), 0) + torow("pt", LW * (3 - slot), 1)
+            if t == 4:
+                for k in range(3):
+                    mm(ap("p4", 0, 256), ident(I1), lst("bt", k), k == 0, k == 2)
+                act(lst("bt", BASE), ap("p4", 0, 256), F.Identity, bias=1.0)
+                items += torow("bt", LW * BASE, 5)
             if t == 5:
-                act(ap("bt", 6 * LW, 6 * LW + 256), ap("p4", 0, 256), F.Copy)
-                dmas("y", torow("bt", 6 * LW, 6, (0, 1)))
-        calls = {"y": void, "n": count, "x": nexts, "k": crash, "m": mx, "a": ypsum, "d": dpsum, "e": dafter,
-                 "D": dpsum, "R": rise, "b": addx, "M": mxs, "F": fused, "A": adddma,
-                 "j1": j1, "j2": j2, "j3": j3, "j4": j4, "q0": q0, "q1": q1, "u5": c5, "up": update}
-        either = {"g": g1, "h": g2, "c": cmp_, "p": cmpf, "l": relu, "z": own}
-        for w in order:
-            if w in calls:
-                calls[w]()
-            elif w[0] in calls:
-                calls[w[0]](int(w[1:]))
-            else:
-                either[w[0].lower()]("v" if w[0].islower() else "s", int(w[1:]))
-        ts(b, ap("p2", 0, 256), ap("sc", 0, 1), A.is_lt)
-        mm(ap("p0", 0, 256), ident(I4096), b, False, True)
-        if names and not last:
-            ts(ap("rw"), b, BIG, A.mult, -BIG / 2, A.add)
-            tt(ap("nbe"), ap("p3", 0, 256), ap("rw"), A.is_gt)
-        if not last:
-            dmas("y", torow("bt", LW * (t - 1), 2, (0,)) + torow("bt", LW * (t - 1), 3 + t % 2, (1,)))
-        ts(ap("idx"), ap("p0", 0, 256), col(PM), A.add)
+                act(lst("bt", C5), ap("p4", 0, 256), F.Copy)
+                items += torow("bt", LW * C5, 6) + torow("bt", LW * 3, 7)
+            dmas("y", items)
 
-        def address():
-            if last:
-                ts(ap("rw"), b, BIG, A.mult, -BIG / 2, A.add)
-                tt(ap("nbe"), ap("p3", 0, 256), ap("rw"), A.is_gt)
-            tt(ap("p3", 256, 512), ap("p3", 0, 256), ap("nbe"), A.mult)
-            tt(ap("p3", 0, 256), ap("p3", 256, 512), ap("s0"), A.add)
-        if not last:
-            sv = SEL_V if names else SEL_V_FIRST
-            lo = V + GH - sv
-            cuts = [GH] + [c for c in (1024, 2048, 3072) if c < lo - 256] + [lo]
-            for c0, c1 in zip(cuts, cuts[1:]):
-                sel("s", c0, c1)
-            if names:
-                address()
-                s = ap("p3", 0, 256)
-                pt, pj = ap("pt", LW * slot, LW * slot + 256), ap("pj", LW * slot, LW * slot + 256)
+        def address(k):
+            s = ap("p5", 0, 256)
+            pt, pj = lst("pt", slot), lst("pj", slot)
+            if k == 0:
+                tt(ap("nbe"), ap("p3", 0, 256), b, A.is_gt)
+            elif k == 1:
+                tt(ap("tf"), ap("p3", 0, 256), ap("nbe"), A.mult)
+                mm(s, ident(I1), lst("pt"), True, False)
+                mm(s, ident(I1), lst("pj"), False, False)
+                mm(s, ident(INH), ap("nbe"), False, False)
+                mm(s, ap("i32"), ap("tf"), False, True)
+            elif last:
+                ts(ap("oa"), s, 16.0, A.mult, 16 * S0, A.add)
+                dmas("y", store("ya", "oa", 0, 256))
+            elif k == 2:
                 ts(pt, s, MAGIC, A.add, MAGIC, A.subtract)
-                ts(ap("of1"), s, S0, A.add)
+            elif k == 3:
                 tt(pj, s, pt, A.subtract)
                 mm(ap("p1", 0, 256), ident(I4864), ap("nbe"), True, False)
                 mm(ap("p1", 0, 256), ident(I16TH), pt, False, False)
                 mm(ap("p1", 0, 256), ident(I304), pj, False, True)
-                sel("v", lo, lo + 512)
-                ts(ap("of2"), ap("p1", 0, 256), 2408.0, A.add)
-                sel("v", lo + 512, V)
+            elif k == 4:
+                ts(ap("of1"), s, S0, A.add)
             else:
-                sel("v", lo, V)
-        else:
-            mm(ap("p4", 0, 256), ident(IHUGE), b, False, True)
-            for k in range(STEPS):
-                mm(ap("p5", 0, 256), ident(I1), ap("bt", LW * k, LW * k + 256), k == 0, k == STEPS - 1)
-            ts(ap("ou"), ap("p4", 0, 256), 16 * S0, A.add, -1.0, A.max)
-            dmas("y", store("yu", "ou", 0, 256))
-            for k, (c0, c1) in enumerate(zip(LAST_CUTS, LAST_CUTS[1:])):
-                sel("sv"[k % 2], c0, c1)
-                dmas("y", store("yx", nxt, c0, c1))
-                if k == 0:
-                    act(ap("oi"), ap("p5", 0, 256), F.Identity, bias=1.0)
-                    dmas("y", store("yi", "oi", 0, 256))
-                if k == 3:
-                    address()
-                    ts(ap("oa"), ap("p3", 0, 256), 16.0, A.mult, 16 * S0, A.add)
-            dmas("y", store("ya", "oa", 0, 256))
+                ts(ap("of2"), ap("p1", 0, 256), 2408.0, A.add)
+
+        def output(k):
+            if k == 0:
+                mm(ap("p4", 0, 256), ident(IHUGE), b, False, True)
+                ts(ap("ou"), ap("p4", 0, 256), 16 * S0, A.add, -1.0, A.max)
+                dmas("y", store("yu", "ou", 0, 256))
+            else:
+                for j in range(STEPS):
+                    mm(ap("p1", 0, 256), ident(I1), lst("bt", j), j == 0, j == STEPS - 1)
+                act(ap("oi"), ap("p1", 0, 256), F.Identity, bias=1.0)
+                dmas("y", store("yi", "oi", 0, 256))
+
+        whole = {"X": opennames, "y": void, "up": update, "D": maxima, "later": later, "W": spread, "fs": lambda: act(ap("mw", 4 * CH, 6 * CH), ap("mw", 0, 2 * CH), F.Copy), "ag": ghosty, "mg": ghostmax}
+        calls = {"w": againdma, "f": lambda k: fill(ap("mw", 2 * CH * k, 2 * CH * (k + 1)), 0.0), "J": judges, "j": lambda k: part(0, k), "k": lambda k: part(1, k), "K": lambda k: part(2, k), "n": count, "x": nexts, "m": mx, "a": ypsum, "d": dpsum, "R": rise, "b": addx, "M": mxs, "F": fused,
+                 "A": adddma, "z": own, "Z": gtwin, "u": address, "o": output}
+        either = {"g": g1, "h": g2, "c": cmp_, "p": cmpf, "l": relu, "i": relu2, "t": twin, "e": ghosts, "q": again}
+
+        def call(w):
+            q = "v" if w[0].islower() else "s"
+            if w in whole:
+                whole[w]()
+            elif w[0] in calls:
+                calls[w[0]](int(w[1:]))
+            elif w[0] == "O":
+                dmas("y", store("yx", nxt, 256 * int(w[1], 17), 256 * int(w[2], 17)))
+            elif w[0] in "sS":
+                sel(q, w[1:])
+            else:
+                either[w[0].lower()](q, int(w[1:]))
+        return order, call
+
+    steps = {t: step(t) for t in range(1, STEPS + 1)}
+    for t in steps:
+        for w in steps[t][0]:
+            if w[-1] == "+":
+                steps[t + 1][1](w[:-1])
+            else:
+                steps[t][1](w)
 
     def meet(a, c):
         return a[0] == c[0] and a[1] < c[2] and c[1] < a[2] and (a[3] is None or c[3] is None or a[3] == c[3])

from concourse.bass import DstId, RemoteDMATransfer
from concourse.mybir import AluOpType, AxisListType, ActivationFunctionType

A = AluOpType
F = ActivationFunctionType
V, GH, W, STEPS, N = 4096, 256, 4864, 6, 4
LW = W // 16
CH = 1024
BIG = 16384.0
MAGIC = 201326592.0
S0 = 2055.5
U = 1.0 / 16384

SCRATCH = {
    "xa": ("sbuf", [128, W], "bfloat16"), "xb": ("sbuf", [128, W], "bfloat16"),
    "gw": ("sbuf", [128, 6 * CH], "bfloat16"), "gx": ("sbuf", [128, 96], "uint16"),
    "w2": ("sbuf", [128, 3 * V], "bfloat16"), "mw": ("sbuf", [128, 2 * W], "bfloat16"),
    "dd": ("sbuf", [128, V], "bfloat16"), "cm": ("sbuf", [128, V], "bfloat16"),
    "rr": ("sbuf", [128, V], "bfloat16"), "xo": ("sbuf", [128, V], "bfloat16"), "go": ("sbuf", [128, V], "bfloat16"),
    "adi": ("sbuf", [128, 256], "int32"), "sgi": ("sbuf", [128, 288], "int32"), "lmi": ("sbuf", [128, 288], "int32"),
    "of1": ("sbuf", [128, 256], "uint16"), "of2": ("sbuf", [128, 256], "uint16"), "idx": ("sbuf", [128, 256], "uint16"),
    "ofc": ("sbuf", [128, 16], "uint16"),
    "s0": ("sbuf", [128, 256], "float32"), "tf": ("sbuf", [128, 256], "float32"), "i32": ("sbuf", [128, 128], "float32"),
    "pt": ("sbuf", [128, 3 * LW], "bfloat16"), "pj": ("sbuf", [128, 3 * LW], "bfloat16"),
    "bt": ("sbuf", [128, 8 * LW], "bfloat16"),
    "cr": ("sbuf", [128, 256], "bfloat16"), "nbe": ("sbuf", [128, 256], "bfloat16"), "k16": ("sbuf", [128, 256], "bfloat16"),
    "d1": ("sbuf", [128, 256], "bfloat16"), "n2": ("sbuf", [128, 256], "bfloat16"), "zs": ("sbuf", [128, 256], "bfloat16"),
    "seg": ("sbuf", [128, 256], "bfloat16"), "dec": ("sbuf", [128, 256], "bfloat16"), "rw": ("sbuf", [128, 256], "bfloat16"),
    "ic": ("sbuf", [128, 144], "bfloat16"), "icf": ("sbuf", [128, 16], "float32"), "pi": ("sbuf", [128, 4], "int32"),
    "col": ("sbuf", [128, 32], "float32"), "oh": ("sbuf", [128, 16], "float32"),
    "bs": ("sbuf", [128, 6 * 144], "bfloat16"), "ids": ("sbuf", [128, 11 * 128], "bfloat16"),
    "ms": ("sbuf", [128, 6 * 128], "bfloat16"),
    "jf": ("sbuf", [128, 3 * 256], "bfloat16"), "js": ("sbuf", [128, 64], "bfloat16"), "th": ("sbuf", [128, 64], "float32"),
    "up": ("sbuf", [128, 80], "bfloat16"), "bp": ("sbuf", [128, 256], "bfloat16"), "kq": ("sbuf", [128, 16], "bfloat16"), "ed": ("sbuf", [128, 8], "bfloat16"),
    "sc": ("sbuf", [128, 4], "float32"), "v0": ("sbuf", [128, 32], "float32"), "ix0": ("sbuf", [128, 16], "uint16"),
    "oa": ("sbuf", [128, 256], "float32"), "ou": ("sbuf", [128, 256], "float32"), "oi": ("sbuf", [128, 256], "float32"),
}
for _k in range(8):
    SCRATCH["p%d" % _k] = ("psum", [128, 512], "float32")
NDMA = 90
SEMAPHORES = ["qv", "qs", "qt", "qg"] + ["dm%d" % k for k in range(NDMA)] + ["ar%d" % k for k in range(2 * STEPS)] + ["lo%d" % k for k in range(2 * STEPS)]

ORDER = {
    1: "later G2 F0 d4 d5 X+ F1 p0 L0 C4 R4 R5 C5 L1 n0 ag n2 F3 p1 n1 w0 w2 w3 w1 A0 A2 A1 p3 n3 mg j0 k0 j1 k1 K2 K3 K4 K5 J0 I6 K6 J1 K7 J2 i7 b7 b6 up K9 S01 J5 J3 K8 M7 M6 Sac Scg s8a s14 s48 Z0 z1 Z3 h0+ h2+ x0+ H1+ H3+ x1+ x2+ x3+",
    2: "G2 F0 up F1 p0 L0 d4 d5 C4 C5 R5 P1 R4 n0 n2 n1 ag F3 A0 A2 p3 n3 j0 mg k0 j1 k1 K2 K3 K4 K5 J0 L1 I7 I6 b7 b6 K6 J1 A1 K7 J2 K9 J3 K8 u0 u1 s14 u4 u2 X+ u3 u5 h0+ h2+ M6 M7 S01 J5 Scg Sac S48 S8a z0 Z3 Z1 x0+ H3+ H1+ x1+ x2+ x3+",
    0: "G2 F0 y d4 C4 up d5 C5 L0 F1 p0 n0 n2 ag F3 p1 A0 n1 L1 R4 R5 I7 I6 A1 p3 mg n3 j0 k0 j1 k1 K2 K3 K4 J0 K5 b7 K6 J1 K7 J2 J3 K9 M7 b6 S01 M6 J5 A2 u0 K8 u1 s14 u2 Scg S48 u3 u4 u5 h0+ h2+ X+ sac H1+ S8a H3+ z0 Z3 Z1 x0+ x1+ x2+ x3+",
    6: "G2 F0 d4 d5 L0 C4 y C5 F1 p0 l1 F3 n0 p3 n2 P1 R4 R5 A0 A1 A2 n1 n3 j0 L3 A3 k0 j1 k1 K2 K3 K4 J0 K5 K6 J1 K7 J2 J3 K8 u0 o0 S04 o1 u1 s48 O08 u2 scg S8c O8g",
}


def rank_program(g, core, T, topo):
    rank = T.rank_of(core)
    if rank is None:
        return
    ops = []
    Q = {"v": g.vector, "s": g.scalar, "t": g.tensor, "g": g, "y": g.sync}

    def ap(name, c0=0, c1=None, step=1, p=128):
        t = T[name]
        c1 = t.shape[1] if c1 is None else c1
        a = t[0:p, c0:c1:step] if step > 1 else t[0:p, c0:c1]
        if name[0] == "p" and name[1].isdigit():
            return a, [(name, 0, 512, None)]
        return a, [(name, c0, c1, None)]

    def ind(win, off):
        return win[0].indirect(off[0]), win[1] + off[1]

    def val(x):
        return x[0] if isinstance(x, tuple) else x

    def reg(*xs):
        r = []
        for x in xs:
            if isinstance(x, tuple):
                r += x[1]
        return r

    def emit(q, fn, rd, wr, kind="c", sem=None, n=0):
        ops.append({"q": q, "fn": fn, "rd": rd, "wr": wr, "kind": kind, "sem": sem, "n": n, "need": False})

    def ts(out, in0, s1, op0, s2=None, op1=None):
        if op1 is None:
            emit("v", lambda: g.vector.tensor_scalar(out[0], in0[0], val(s1), None, op0), reg(in0, s1), out[1])
        else:
            emit("v", lambda: g.vector.tensor_scalar(out[0], in0[0], val(s1), val(s2), op0, op1), reg(in0, s1, s2), out[1])

    def tt(out, in0, in1, op):
        emit("v", lambda: g.vector.tensor_tensor(out[0], in0[0], in1[0], op), reg(in0, in1), out[1])

    def scan(out, d0, d1, op0, op1, first=0.0):
        emit("v", lambda: g.vector.tensor_tensor_scan(out[0], d0[0], d1[0], val(first), op0, op1), reg(d0, d1, first), out[1])

    def cp(out, in0):
        emit("v", lambda: g.vector.tensor_copy(out[0], in0[0]), in0[1], out[1])

    def fill(out, c):
        emit("v", lambda: g.vector.memset(out[0], c), [], out[1])

    def act(out, in0, func, bias=0.0, scale=1.0):
        emit("s", lambda: g.scalar.activation(out[0], in0[0], func, bias=val(bias), scale=scale), reg(in0, bias), out[1])

    def mm(out, l, r, start, stop):
        emit("t", lambda: g.tensor.matmul(out[0], l[0], r[0], start, stop), reg(l, r), out[1])

    def iota(out, pattern, base, cm):
        if out[1][0][0] == "pi":
            emit("g", lambda: g.iota(out[0], pattern, base, cm), [], out[1])
        else:
            emit("g", lambda: g.iota(out[0], pattern, base, cm, allow_small_or_imprecise_dtypes=True), [], out[1])

    nd = [0]

    def dmas(q, items):
        sem = "dm%d" % nd[0]
        nd[0] += 1
        for o, i, rd, wr in items:
            emit(q, (lambda o=o, i=i: Q[q].dma_start(o, i)), rd, wr, "d", sem, 16 * len(items))

    def rot(rows):
        k = rank * rows
        return [(0, k, 8 * rows - k), (8 * rows - k, 0, k)] if k else [(0, 0, 8 * rows)]

    def load(name, c0, src, s0, s1, rows=16):
        return [(T[name][a:a + n, c0:c0 + s1 - s0], T[src][b:b + n, s0:s1], [], [(name, c0, c0 + s1 - s0, ("ld", a))]) for a, b, n in rot(rows)]

    def store(dst, name, c0, c1):
        return [(T[dst][b:b + n, c0:c1], T[name][a:a + n, c0:c1], [(name, c0, c1, None)], []) for a, b, n in rot(16)]

    def torow(name, c0, row, regions=(0, 1)):
        return [(T.mw[row:128:16, r * W:(r + 1) * W], T[name][:, c0:c0 + LW], [(name, c0, c0 + LW, None)], [("mw", r * W, (r + 1) * W, row)]) for r in regions]

    peers = [T.cores[(rank + d) % N] for d in range(1, N)]
    mask = topo.mask(core, peers[0])
    for c in peers[1:]:
        mask &= topo.mask(core, c)
    neng = bin(mask).count("1")

    ns = [0]

    def send(src, dsts):
        k = ns[0]
        ns[0] += 1
        ids = [DstId(rid=topo.addr(c)[0], pnc=topo.addr(c)[1]) for c in peers]
        emit("g", lambda: g.remote_dma_fused([RemoteDMATransfer(dst_ids=ids, dma_engine_mask=mask, remote_sem=T.sem["ar%d" % k],
                                                                src=src[0], dsts=[d[0] for d in dsts])], local_sem=T.sem["lo%d" % k]),
             src[1], [], "r", "lo%d" % k, neng)
        emit("x", None, [], reg(*dsts), "a", "ar%d" % k, neng * (N - 1))

    def gblock(k, d, n=1):
        return ap("gw", CH * k + GH * d, CH * k + GH * (d + n))

    def goffs(t, d):
        return ap("gx", 16 * (3 * (t % 2) + d), 16 * (3 * (t % 2) + d + 1))

    def col(k):
        return ap("col", k, k + 1)

    def oh(k):
        return ap("oh", k, k + 1)

    def bmat(k, j):
        return ap("bs", 144 * k + 15 - j, 144 * k + 143 - j)

    def ident(k):
        return ap("ids", 128 * k, 128 * k + 128)

    def mat(k, p=128):
        return ap("ms", 128 * k, 128 * k + 128, p=p)

    def lst(name, k=0, c0=0, c1=256):
        return ap(name, LW * k + c0, LW * k + c1)

    def mcol(k):
        return 3 * CH * (k // 2) + 512 * (k % 2)

    B1, BH, BU, BU6, BC5, BC6 = range(6)
    I1, INEG, ICH, I304, I16TH, I4864, INU, INH, I16, IHUGE = range(10)
    BLK, SCO, ALL, E8, MGE, MTMP = range(6)
    P, PM, C0, C15, G0, WA, WB, WC, WD, WE, JJ, NB, N3, VB, SC = range(15)
    LIM, TH, TMP = 0, 256, 512
    NE, THR, LM = 0, 17, 34
    D2, E2, W3, RQ, M13 = range(0, 80, 16)
    C5, BASE = 6, 7

    dmas("y", load("xa", 0, "x0", 0, GH))
    dmas("s", load("sgi", 0, "sg", 0, 273, 1) + load("lmi", 0, "lm", 0, 273, 1))
    dmas("y", load("adi", 0, "ad", 0, 256))
    dmas("y", load("xa", GH, "x0", GH, V // 2))
    dmas("y", load("xa", V // 2, "x0", V // 2, V))
    iota(ap("ic"), [[1, 144]], 0, 0)
    iota(ap("pi", 0, 1), [[1, 1]], 0, 1)
    iota(col(G0), [[1, 1]], 0, 16)
    iota(mat(MGE), [[16, 8], [0, 16]], 0, 0)
    iota(ap("pt", 256, LW), [[16, 48]], 2048, 0)
    send(ap("xa", 0, GH), [ap("xa", V + d * GH, V + (d + 1) * GH) for d in range(N - 1)])
    iota(ap("k16"), [[0, 4], [16, 64]], 0, 0)
    iota(ap("mw", 2 * V, 2 * W), [[0, 2 * (W - V)]], 0, 0)
    cp(col(P), ap("pi", 0, 1))
    ts(ap("pi", 1, 2), ap("pi", 0, 1), 15, A.bitwise_and)
    ts(ident(I1), ap("ic", 0, 128), col(P), A.is_equal)
    fill(col(WE), 1.0 / 64)
    cp(col(PM), ap("pi", 1, 2))
    cp(ap("icf"), ap("ic", 0, 16))
    for k, w in ((INEG, -1.0), (ICH, float(CH)), (I304, float(LW)), (I16TH, 0.0625)):
        act(ident(k), ident(I1), F.Copy, scale=w)
    act(mat(ALL), ident(I16TH), F.Identity, bias=col(WE), scale=0.0)
    fill(col(NB), -16.5)
    tt(col(C0), col(P), col(PM), A.subtract)
    fill(ap("seg"), 1.0)
    ts(col(C15), col(C0), 15.0, A.add)
    cp(ap("ofc"), ap("icf"))
    fill(ap("seg", 0, 256, 16), 0.0)
    ts(ap("bs", 0, 144), ap("ic"), col(C15), A.is_equal)
    ts(ap("bs", 144 * BH, 144 * BH + 144), ap("ic"), col(C15), A.is_equal, 0.5, A.mult)
    ts(col(JJ), col(PM), -7.5, A.add)
    act(lst("pj", 0, 256, LW), ap("ic", 0, 48), F.Identity, bias=col(JJ), scale=0.0)
    act(lst("bt", 0, 256, LW), ap("ic", 0, 48), F.Copy, scale=0.0)
    for k in (1, 2):
        act(lst("pj", k, 256, LW), lst("pj", 0, 256, LW), F.Copy)
        act(lst("pt", k, 256, LW), lst("pt", 0, 256, LW), F.Copy)
    for k in (1, 2, 3, 4, BASE):
        act(lst("bt", k, 256, LW), lst("bt", 0, 256, LW), F.Copy)
    for k, w in ((I4864, float(W)), (INH, -BIG / 2), (INU, -U), (I16, 16.0), (IHUGE, -131072.0)):
        act(ident(k), ident(I1), F.Copy, scale=w)
    act(ap("i32"), ident(I1), F.Copy, scale=BIG)
    ts(mat(MTMP), ap("ic", 0, 128), col(P), A.is_ge, 32.0, A.mult)
    ts(mat(E8), mat(MGE), col(G0), A.is_equal)
    ts(ap("js", NE, NE + 17, p=8), ap("sgi", 256, 273, p=8), 1.0, A.not_equal)
    tt(mat(MTMP), mat(MTMP), ident(ICH), A.add)
    ts(ap("js", THR, THR + 17, p=8), ap("sgi", 256, 273, p=8), 2.0, A.not_equal)
    ts(ap("js", LM, LM + 17, p=8), ap("lmi", 256, 273, p=8), 0.0, A.add)
    ts(mat(MTMP), mat(MTMP), 1.0, A.add, -U, A.mult)
    ts(mat(BLK), mat(MGE), col(C0), A.is_equal)
    tt(ap("js", THR, THR + 17, p=8), ap("js", THR, THR + 17, p=8), ap("js", LM, LM + 17, p=8), A.mult)
    ts(ap("jf", TMP, TMP + 256, p=8), ap("sgi", 0, 256, p=8), -500.0, A.mult, -519.5, A.max)
    tt(mat(SCO), mat(MTMP), mat(BLK), A.mult)
    mm(ap("p1", 0, 51), mat(E8, 8), ap("js", 0, 51, p=8), True, True)
    ts(ap("jf", LIM, LIM + 256, p=8), ap("lmi", 0, 256, p=8), -1.0, A.mult, -0.5, A.add)
    ts(ap("jf", TH, TH + 256, p=8), ap("jf", TMP, TMP + 256, p=8), 520.0, A.add, U, A.mult)
    cp(ap("of1"), ap("adi"))
    act(ap("th", 0, 51), ap("p1", 0, 51), F.Copy, scale=0.0625)
    ts(ap("s0"), ap("adi"), -S0, A.add)
    ts(ap("oh"), ap("icf"), col(PM), A.is_equal)
    ts(ap("dec"), ind(ap("th", 0, 16), ap("ofc")), -1.0, A.mult)
    ts(ap("up", M13, M13 + 16), ap("icf"), 0.0, A.mult, ap("th", NE + 16, NE + 17), A.is_equal)
    fill(ap("dec", 0, 256, 16), -99.0)
    first = ORDER[1].split()
    for c in range(4):
        if "F%d" % c in first:
            act(ap("xo", CH * c, CH * c + CH), ap("xa", CH * c, CH * c + CH), F.Copy)
    def initial(c):
        dmas("y", [(o, i, [("xa", GH, V, None)], wr) for o, i, rd, wr in load("w2", mcol(2 * c) + CH, "xi", CH * c, CH * c + CH)])
    for c in range(4):
        initial(c)
    if "mg" in first:
        dmas("y", [(o, i, [("xa", GH, V, None)], wr) for k in (1, 2) for o, i, rd, wr in load("gw", k * GH, "xi", 0, GH)])
        ts(ap("v0", 0, 16), ap("icf"), 16.0, A.mult, col(PM), A.add)
        act(ap("kq"), ap("v0", 0, 16), F.Copy, scale=4.0)
        fill(ap("w2", 0, GH), 0.0)
    if "D" in first:
        for k in (0, 1, 3, 4):
            iota(gblock(k, 3), [[0, GH]], 0, 0)
        send(ap("w2", CH, CH + GH), [gblock(4, d) for d in range(N - 1)])

    def spread():
        dmas("y", [(gblock(k, 0, 3)[0], gblock(4, 0, 3)[0], gblock(4, 0, 3)[1], gblock(k, 0, 3)[1]) for k in (5, 1, 2)])

    ts(lst("pt"), ap("s0"), MAGIC, A.add, MAGIC, A.subtract)
    ts(col(WB), oh(3), oh(4), A.add, -2.0, A.mult)
    ts(col(WE), oh(0), oh(1), A.add, U, A.mult)
    tt(lst("pj"), ap("s0"), lst("pt"), A.subtract)
    ts(col(WC), col(WB), oh(2), A.subtract, col(WE), A.add)
    fill(col(VB), -64.0)
    fill(ap("jf", TMP, TMP + 256, p=8), 0.5)
    mm(ap("p5", 0, 256), ident(I304), lst("pj"), True, False)
    mm(ap("p5", 0, 256), ident(I16TH), lst("pt"), False, True)
    ts(ap("bs", 144 * BU, 144 * BU + 144), ap("ic"), col(C15), A.is_equal, col(WC), A.mult)
    ts(ap("of2"), ap("p5", 0, 256), 2408.0, A.add)
    act(lst("bt", C5, 0, LW), ap("xa", 0, LW), F.Copy, scale=0.0)

    def later():
        ts(col(WB), oh(6), U / 16, A.mult, col(WC), A.add)
        ts(col(WD), oh(2), oh(5), A.add)
        ts(col(WE), oh(7), col(WD), A.add)
        for k, w in ((BU6, WB), (BC5, WD), (BC6, WE)):
            ts(ap("bs", 144 * k, 144 * k + 144), ap("ic"), col(C15), A.is_equal, col(w), A.mult)

    def step(t):
        cur, nxt = ("xa", "xb")[(t - 1) % 2], ("xa", "xb")[t % 2]
        names, raw, last = t > 1, t > 2, t == STEPS
        order = ORDER.get(t, ORDER[0]).split()
        signs = [c for c in range(4) if "C%d" % (2 * c) in order or "P%d" % c in order]
        slot = 1 + (t % 2)
        b = lst("bt", t - 1)

        def wide(name, c0, c1, st=1):
            if t == 1 and name in ("cm", "dd"):
                o = V if name == "dd" else 0
                return ap("mw", o + c0, o + c1, st)
            return ap(name, c0, c1, st)

        def again(q, c):
            gather(q, ap("w2", mcol(2 * c) + 2 * CH, mcol(2 * c) + 3 * CH), ap("w2", mcol(2 * c) + CH, mcol(2 * c) + 2 * CH))

        def againdma(c):
            o, i = ap("w2", mcol(2 * c) + 2 * CH, mcol(2 * c) + 3 * CH), ap("w2", mcol(2 * c) + CH, mcol(2 * c) + 2 * CH)
            dmas("y", [(o[0], i[0], i[1], o[1])])

        def chunk(name, c):
            return wide(name, CH * c, CH * c + CH)

        def half(name, k):
            return wide(name, 512 * k, 512 * k + 512)

        def gather(q, o, i):
            if q == "v":
                cp(o, i)
            else:
                act(o, i, F.Copy)

        def g1(q, c):
            gather(q, chunk("dd", c), ind(ap(cur), ap("of1", 64 * c, 64 * c + 64)))

        def g2(q, c):
            gather(q, chunk("go", c), ind(ap("mw"), ap("of2", 64 * c, 64 * c + 64)))

        def own(c):
            o, i = chunk("xo", c), chunk(nxt, c)
            dmas("y", [(o[0], i[0], i[1], o[1])])

        def fused(c):
            tt(chunk("dd", c), ind(ap(cur), ap("of1", 64 * c, 64 * c + 64)), chunk("xo", c), A.subtract)

        def compare(q, o, i):
            if q == "s":
                act(o, i, F.Sign, bias=col(NB), scale=-1.0)
            else:
                ts(o, i, -16.5, A.is_lt, 0.5, A.subtract)

        def cmpf(q, c):
            compare(q, chunk("cm", c), chunk("dd", c))

        def relu(q, c):
            c0 = GH if c == 0 and "mg" in order else 0
            o, i = ap("w2", mcol(2 * c) + c0, mcol(2 * c) + CH), wide("dd", CH * c + c0, CH * c + CH)
            if q == "s":
                act(o, i, F.Relu)
            else:
                ts(o, i, 0.0, A.max)

        def ghosty():
            mm(ap("p5", 0, GH), ident(I1), ap(cur, 0, GH), True, False)
            mm(ap("p5", 0, GH), ident(I1), wide("dd", 0, GH), False, True)

        def ghostmax():
            tt(ap("gw", 0, GH), ap("p5", 0, GH), ap(cur, 0, GH), A.max)

        def relu2(q, k):
            if q == "s":
                act(half("rr", k), half("dd", k), F.Relu)
            else:
                ts(half("rr", k), half("dd", k), 0.0, A.max)

        def twin(q, c):
            gather(q, chunk("xo", c), chunk(nxt, c))

        def gtwin(c):
            o, i = chunk("xo", c), chunk(nxt, c)
            emit("g", lambda: g.affine_select(o[0], i[0], [[0, CH]], A.is_gt, 0.0, 1, 0), i[1], o[1])

        def adddma(c):
            c0 = GH if c == 0 and "mg" in order else 0
            o, i = ap("w2", mcol(2 * c) + c0, mcol(2 * c) + CH), ap(cur, CH * c + c0, CH * c + CH)
            sem = "dm%d" % nd[0]
            nd[0] += 1
            emit("g", lambda: g.dma_start(o[0], i[0], accum_op=A.add), i[1] + o[1], o[1], "d", sem, 16)

        def bank(kind, k):
            return ap("p%d" % (6 + k % 2))

        def ypsum(k):
            if "F%d" % (k // 2) in order:
                mm(bank("y", k), ident(I1), half(cur, k), True, False)
                mm(bank("y", k), ident(I1), half("dd", k), False, True)
            else:
                mm(bank("y", k), ident(I1), half("dd", k), True, True)

        def mx(k):
            tt(ap("w2", mcol(k), mcol(k) + 512), bank("y", k), half(cur, k), A.max)

        def dpsum(k):
            mm(bank("d", k), ident(INEG), half(cur, k), True, False)
            mm(bank("d", k), ident(I1), half("dd", k), False, True)

        def cmp_(q, k):
            compare(q, half("cm", k), bank("d", k))

        def rise(k):
            o = ap("w2", mcol(k), mcol(k) + 512) if "A%d" % (k // 2) in order else half("rr", k)
            act(o, bank("d", k), F.Relu)

        def addx(k):
            mm(bank("y", k), ident(I1), half(cur, k), True, False)
            mm(bank("y", k), ident(I1), half("rr", k), False, True)

        def mxs(k):
            act(ap("w2", mcol(k), mcol(k) + 512), bank("y", k), F.Copy)

        def pick(out, k, src, c, start, stop):
            for j in range(16):
                mm(out, bmat(k, j), wide(src, CH * c + j, CH * c + CH, 16), start and j == 0, stop and j == 15)

        def opennames():
            mm(ap("p3", 0, 256), ident(INU), lst("pt"), True, False)
            mm(ap("p3", 0, 256), ident(INU), lst("pj"), False, False)
            mm(ap("p3", 0, 256), mat(E8, 8), ap("jf", TMP, TMP + 256, p=8), False, False)
            if t == 5:
                mm(ap("p4", 0, 256), ident(I1), lst("bt", C5), True, False)
            if last:
                mm(ap("p4", 0, 256), ident(I16), lst("pt", 3 - slot), True, False)
                mm(ap("p4", 0, 256), ident(I16), lst("pj", 3 - slot), False, False)

        picked = []

        def nexts(c):
            picked.append(c)
            pick(ap("p3", 64 * c, 64 * c + 64), BU6 if last else BU, "go", c, False, len(picked) == 4)
            if t >= 5:
                pick(ap("p4", 64 * c, 64 * c + 64), BC6 if last else BC5, "go", c, False, t == 5 and len(picked) == 4)

        def void():
            act(ap("rw"), ap("p3", 0, 256), F.Relu, bias=col(VB), scale=-64.0)

        def count(c):
            o = ap("p0", 64 * c, 64 * c + 64) if c < 3 else ap("p1", 0, 64)
            pick(o, BH if c in signs else B1, "cm", c, True, not raw)
            if raw:
                mm(o, ident(I1), ap("rw", 64 * c, 64 * c + 64), False, True)

        def part(h, k):
            c0, c1 = ((0, 192), (192, 256), (0, 256))[h]
            n = c1 - c0
            cnt, n1, score, at = ((ap("p0", 0, n), ap("p0", 256, 256 + n), ap("p2", 0, n), ap("p0", 0, n)) if h != 1 else
                                  (ap("p1", 0, n), ap("p1", 64, 64 + n), ap("p1", 128, 128 + n), ap("p1", 192, 192 + n)))
            if h == 1 and "K7" in order:
                score = ap("p2", c0, c1)
            tot, head = ap("n2", c0 + 15, c1, 16), ap("d1", c0, c1, 16)

            def u(c, name="up"):
                return ap(name, c + c0 // 16, c + c1 // 16)
            if k == 0:
                ts(ap("cr", c0, c1), cnt, 0.5, A.is_gt)
                mm(n1, mat(E8, 8), ap("jf", LIM + c0, LIM + c1, p=8), True, False)
                mm(n1, mat(BLK), ap("cr", c0, c1), False, True)
                mm(score, mat(E8, 8), ap("jf", TH + c0, TH + c1, p=8), True, False)
                mm(score, mat(SCO), ap("cr", c0, c1), False, True)
            elif k == 1:
                ts(ap("d1", c0, c1), n1, 0.0, A.is_gt, 0.0625, A.mult)
            elif k == 2:
                scan(ap("n2", c0, c1), ap("seg", c0, c1), ap("d1", c0, c1), A.mult, A.add)
            elif k == 3:
                tt(u(D2), tot, u(LM, "th"), A.is_gt)
                tt(u(E2), tot, u(THR, "th"), A.is_gt)
            elif k == 4:
                scan(u(W3), u(M13), u(D2), A.mult, A.add, ap("up", W3 + 11, W3 + 12) if h == 1 else 0.0)
                tt(u(RQ), u(E2), head, A.max)
            elif k == 5:
                tt(head, u(W3), u(RQ), A.max)
            elif k == 6:
                scan(ap("zs", c0, c1), ap("dec", c0, c1), ap("d1", c0, c1), A.add, A.max)
            elif k == 7:
                tt(ap("bp", c0, c1), score, ap("zs", c0, c1), A.is_lt)
                if h != 1 and "mg" in order:
                    mm(ap("p0", 448, 464), ident(I1), ap("kq"), True, False)
                    mm(ap("p0", 448, 464), ident(ICH), ap("bp", 0, 16), False, True)
                mm(at, ident(I1), ap("k16", c0, c1), True, False)
                mm(at, ident(ICH), ap("bp", c0, c1), False, True)
            elif k == 8:
                e = 16 if h != 1 and ("j9" in order or "K9" in order) else 0
                ts(ap("idx", c0 + e, c1), ap(at[1][0][0], e + 192 * (h == 1), n + 192 * (h == 1)), col(PM), A.add, col(SC), A.add)
            else:
                ts(ap("ix0"), ap("p0", 448, 464), col(SC), A.add, 0.25, A.mult)

        def judges(k):
            def u(c):
                return ap("up", c, c + 16)
            whole_ = ap("p1" if "K7" in order else "p2", 256, 257)
            if k == 0:
                emit("v", lambda: g.vector.tensor_reduce(col(N3)[0], u(D2)[0], AxisListType.X, A.add), u(D2)[1], col(N3)[1])
            elif k == 1:
                ts(ap("ed", 0, 2), ap("th", THR + 16, LM + 17, 17), 16.0, A.mult, col(N3), A.is_lt)
                mm(whole_, mat(ALL), ap("ed", 1, 2), True, False)
                mm(whole_, ident(I1), ap("ed", 0, 1), False, True)
            elif k == 2:
                ts(col(SC), whole_, 0.875, A.is_gt, float(CH), A.mult)
            elif k == 3:
                ts(b, ap("bp"), col(SC), A.add, 0.5, A.is_gt)
                if not last:
                    dmas("y", torow("bt", LW * (t - 1), 2, (0,)) + torow("bt", LW * (t - 1), 3 + t % 2, (1,)))
            elif k == 4:
                send(ap("idx", 0, 16), [goffs(t, d) for d in range(N - 1)])
            else:
                send(ap(nxt, 0, GH), [ap(nxt, V + d * GH, V + (d + 1) * GH) for d in range(N - 1)])

        def maxima():
            send(ap("w2", 0, GH), [gblock(3 * (t % 2), d) for d in range(N - 1)])

        def ghosts(q, d):
            c0 = 3 * CH * (t % 2) + GH * d
            gather(q, ap(nxt, V + GH * d, V + GH * d + GH), ind(ap("gw", c0, c0 + 2 * CH + GH), goffs(t, d)))

        def sel(q, w):
            c0, c1 = 256 * int(w[0], 17), 256 * int(w[1], 17)
            m = mcol(2 * (c0 // CH))
            if c1 == GH and "mg" in order:
                gather(q, ap(nxt, 0, GH), ind(ap("gw", 0, 3 * GH), ap("ix0")))
                return
            gather(q, ap(nxt, c0, c1), ind(ap("w2", m, m + 3 * CH), ap("idx", c0 // 16, c1 // 16)))

        def update():
            if t == 1:
                dmas("y", torow("pj", 0, 0, (0,)) + torow("pt", 0, 1, (0,)) + torow("bt", LW * C5, 3, (0,)) + torow("bt", LW * C5, 4, (0,)))
                return
            if t == 2:
                dmas("y", torow("pj", 0, 0, (1,)) + torow("pt", 0, 1, (1,)) + torow("bt", LW * C5, 2, (1,)))
                return
            items = torow("pj", LW * (3 - slot), 0) + torow("pt", LW * (3 - slot), 1)
            if t == 4:
                for k in range(3):
                    mm(ap("p4", 0, 256), ident(I1), lst("bt", k), k == 0, k == 2)
                act(lst("bt", BASE), ap("p4", 0, 256), F.Identity, bias=1.0)
                items += torow("bt", LW * BASE, 5)
            if t == 5:
                act(lst("bt", C5), ap("p4", 0, 256), F.Copy)
                items += torow("bt", LW * C5, 6) + torow("bt", LW * 3, 7)
            dmas("y", items)

        def address(k):
            s = ap("p5", 0, 256)
            pt, pj = lst("pt", slot), lst("pj", slot)
            if k == 0:
                tt(ap("nbe"), ap("p3", 0, 256), b, A.is_gt)
            elif k == 1:
                tt(ap("tf"), ap("p3", 0, 256), ap("nbe"), A.mult)
                mm(s, ident(I1), lst("pt"), True, False)
                mm(s, ident(I1), lst("pj"), False, False)
                mm(s, ident(INH), ap("nbe"), False, False)
                mm(s, ap("i32"), ap("tf"), False, True)
            elif last:
                ts(ap("oa"), s, 16.0, A.mult, 16 * S0, A.add)
                dmas("y", store("ya", "oa", 0, 256))
            elif k == 2:
                ts(pt, s, MAGIC, A.add, MAGIC, A.subtract)
            elif k == 3:
                tt(pj, s, pt, A.subtract)
                mm(ap("p1", 0, 256), ident(I4864), ap("nbe"), True, False)
                mm(ap("p1", 0, 256), ident(I16TH), pt, False, False)
                mm(ap("p1", 0, 256), ident(I304), pj, False, True)
            elif k == 4:
                ts(ap("of1"), s, S0, A.add)
            else:
                ts(ap("of2"), ap("p1", 0, 256), 2408.0, A.add)

        def output(k):
            if k == 0:
                mm(ap("p4", 0, 256), ident(IHUGE), b, False, True)
                ts(ap("ou"), ap("p4", 0, 256), 16 * S0, A.add, -1.0, A.max)
                dmas("y", store("yu", "ou", 0, 256))
            else:
                for j in range(STEPS):
                    mm(ap("p1", 0, 256), ident(I1), lst("bt", j), j == 0, j == STEPS - 1)
                act(ap("oi"), ap("p1", 0, 256), F.Identity, bias=1.0)
                dmas("y", store("yi", "oi", 0, 256))

        whole = {"X": opennames, "y": void, "up": update, "D": maxima, "later": later, "W": spread, "fs": lambda: act(ap("mw", 4 * CH, 6 * CH), ap("mw", 0, 2 * CH), F.Copy), "ag": ghosty, "mg": ghostmax}
        calls = {"w": againdma, "f": lambda k: fill(ap("mw", 2 * CH * k, 2 * CH * (k + 1)), 0.0), "J": judges, "j": lambda k: part(0, k), "k": lambda k: part(1, k), "K": lambda k: part(2, k), "n": count, "x": nexts, "m": mx, "a": ypsum, "d": dpsum, "R": rise, "b": addx, "M": mxs, "F": fused,
                 "A": adddma, "z": own, "Z": gtwin, "u": address, "o": output}
        either = {"g": g1, "h": g2, "c": cmp_, "p": cmpf, "l": relu, "i": relu2, "t": twin, "e": ghosts, "q": again}

        def call(w):
            q = "v" if w[0].islower() else "s"
            if w in whole:
                whole[w]()
            elif w[0] in calls:
                calls[w[0]](int(w[1:]))
            elif w[0] == "O":
                dmas("y", store("yx", nxt, 256 * int(w[1], 17), 256 * int(w[2], 17)))
            elif w[0] in "sS":
                sel(q, w[1:])
            else:
                either[w[0].lower()](q, int(w[1:]))
        return order, call

    steps = {t: step(t) for t in range(1, STEPS + 1)}
    for t in steps:
        for w in steps[t][0]:
            if w[-1] == "+":
                steps[t + 1][1](w[:-1])
            else:
                steps[t][1](w)

    def meet(a, c):
        return a[0] == c[0] and a[1] < c[2] and c[1] < a[2] and (a[3] is None or c[3] is None or a[3] == c[3])

    hist = {}
    for i, o in enumerate(ops):
        deps = set()
        for rw, regs in (("r", o["rd"]), ("w", o["wr"])):
            for r in regs:
                psum = r[0][0] == "p" and r[0][1].isdigit()
                for (j, rw2, r2) in hist.get(r[0], []):
                    p = ops[j]
                    if j == i or not meet(r, r2):
                        continue
                    same = p["q"] == o["q"] and p["kind"] == "c" and o["kind"] == "c"
                    if rw == "r" and rw2 == "r" and (same or not psum):
                        continue
                    if same and o["q"] == "t":
                        continue
                    if p["kind"] == "d" and o["kind"] == "d" and p["sem"] == o["sem"]:
                        continue
                    deps.add(j)
        o["deps"] = deps if o["kind"] != "a" else set()
        for rw, regs in (("r", o["rd"]), ("w", o["wr"])):
            for r in regs:
                h = hist.setdefault(r[0], [])
                if rw == "w" and r[3] is None:
                    h[:] = [e for e in h if not (e[2][1] >= r[1] and e[2][2] <= r[2])]
                h.append((i, rw, r))
    for o in ops:
        top = {}
        for j in o["deps"]:
            p = ops[j]
            k = p["q"] if p["kind"] == "c" else p["sem"]
            top[k] = max(top.get(k, -1), j)
        o["deps"] = sorted(top.values())
    known = {q: {} for q in Q}
    for i, o in enumerate(ops):
        if o["kind"] == "a":
            o["clock"] = {}
            continue
        kn = known[o["q"]]
        keep = []
        for j in reversed(o["deps"]):
            p = ops[j]
            k = p["q"] if p["kind"] == "c" else p["sem"]
            if kn.get(k, -1) >= (j if p["kind"] == "c" else 0):
                continue
            keep.append(j)
            p["need"] = True
            kn[k] = j if p["kind"] == "c" else 0
            for k2, v2 in p["clock"].items():
                kn[k2] = max(kn.get(k2, -1), v2)
        o["deps"] = keep
        o["clock"] = dict(kn) if o["kind"] == "c" else {}
    count_ = {q: 0 for q in Q}
    waited = {}
    total = {}
    for o in ops:
        if o["kind"] != "c":
            total[o["sem"]] = o["n"]
        if o["kind"] == "a":
            continue
        for j in o["deps"]:
            p = ops[j]
            s, n = ("q" + p["q"], p["at"]) if p["kind"] == "c" else (p["sem"], p["n"])
            Q[o["q"]].wait_ge(T.sem[s], n)
            waited[s] = max(waited.get(s, 0), n)
        r = o["fn"]()
        if o["kind"] == "d":
            r.then_inc(T.sem[o["sem"]], 16)
        elif o["kind"] == "c" and o["need"]:
            count_[o["q"]] += 1
            o["at"] = count_[o["q"]]
            r.then_inc(T.sem["q" + o["q"]], 1)
    for s in total:
        if waited.get(s, 0) < total[s]:
            g.wait_ge(T.sem[s], total[s])
